import numpy as np, ml_dtypes
CORES = [10,34,74,98]
N = 4
BF = ml_dtypes.bfloat16
def gentries(a):
    return np.ascontiguousarray(a.reshape(8, 16, -1).transpose(0, 2, 1)).reshape(8, -1)
def gtable(e):
    e = np.asarray(e); return np.ascontiguousarray(e.reshape(8, -1, 16).transpose(0, 2, 1)).reshape(128, -1).astype(np.int32)
V, S, A, B, T = 1024, 256, 4096, 4, 4
W = V + (N - 1) * S
def parts(rng):
    z = np.exp2(rng.integers(-1, 2, (N, 8, 16, 1))).astype(np.float32); x = {}
    x["h"] = rng.standard_normal((N, 8, 16, V), dtype=np.float32) * z
    x["y"] = rng.standard_normal((N, 8, 16, T), dtype=np.float32) * z
    x["t"] = (z * (0.5 + rng.random(z.shape))).astype(np.float32)
    x["w"] = np.clip(rng.standard_normal((N, 8, 16, A), dtype=np.float32), -2, 2)
    x["M"] = int(rng.integers(0, 60000)) + rng.integers(0, 8, (N, 8, V)); x["m"] = rng.integers(0, A, (N, 8, V))
    x["pd"] = rng.integers(0, W, (N, 8, B, V)); x["lb"] = rng.integers(0, A, (N, 8, B, V)); x["sn"] = rng.integers(0, V, (N, 8, N - 1, S))
    return x
def pack(x):
    def c(a, n):
        v = np.ascontiguousarray(np.reshape(a, (N, 128, n))).astype(np.float32)
        return np.where(np.abs(v) < 2.0 ** -20, np.float32(0), v).astype(np.float32)
    return {"h0": c(x["h"], V), "mt": np.ascontiguousarray(x["M"]).astype(np.int32), "mm": np.ascontiguousarray(x["m"]).astype(np.int32), "wv": c(x["w"], A).astype(BF), "obs": c(x["y"], T), "th": c(x["t"], 1),
            "pd": np.stack([gtable(a.reshape(8, -1)) for a in x["pd"]]), "lb": np.stack([gtable(a.reshape(8, -1)) for a in x["lb"]]), "sn": np.stack([gtable(a.reshape(8, -1)) for a in x["sn"]])}
def at_ends(rng, lo, hi, v, share):
    return np.where(rng.random(v.shape) < share, np.where(rng.random(v.shape) < 0.5, lo, hi), v)
def setup_inputs(rng):
    return pack(parts(rng))
def setup_inputs_spread(rng):
    x = parts(rng)
    x["h"] = rng.standard_normal((N, 8, 16, V), dtype=np.float32) * np.exp2(rng.integers(-3, 3, (N, 8, 1, V))) * (rng.random((N, 8, 1, V)) > 0.0625)
    x["w"] = x["w"] * np.exp2(rng.integers(-4, 1, (N, 8, 1, A))) * (rng.random((N, 8, 1, A)) > 0.0625)
    top = 4096 * int(rng.integers(1, 15)); kind = np.arange(V) & 3
    x["M"] = np.where(kind == 0, top - 1, np.where(kind == 1, top, top - 12 + np.exp2(5 * rng.random((N, 8, V))).astype(np.int64)))
    s, p = x["sn"], x["pd"]; turn = (rng.integers(0, 2, (N, 8, 1, V)) + np.arange(B)[:, None]) & 1
    x["sn"] = s - (s & 3) + (np.arange(S) & 3)
    x["pd"] = np.where(kind == 3, p, p - (p & 3) + np.where(kind == 2, turn, kind))
    return pack(x)
def setup_inputs_ends(rng):
    x = parts(rng)
    x["M"] = 65535 * rng.integers(0, 2, (N, 8, V)); x["M"][:, 5:] = 65535; x["M"][:, 0] = 0
    x["m"] = (A - 1) * rng.integers(0, 2, (N, 8, V)); x["lb"] = at_ends(rng, 0, A - 1, x["lb"], 0.75)
    x["sn"] = at_ends(rng, 0, V - 1, x["sn"], 0.75); x["pd"] = at_ends(rng, 0, W - 1, x["pd"], 0.75)
    x["pd"][:, 7] = at_ends(rng, 0, V - 1, rng.integers(0, V, (N, B, V)), 0.75)
    x["w"] = at_ends(rng, -2, 2, x["w"], 0.7)
    x["t"][:, 0, :15] = 1024; x["t"][:, 7, :15] = 0
    for g in (0, 7):
        x["w"][:, g, 15] = rng.choice(np.array([0, 0, -2, 2]), (N, A)); x["h"][:, g, 15] = rng.choice(np.array([0, 1, -1]), (N, V))
        x["y"][:, g, 15] = 0; x["t"][:, g, 15] = 0
    few = [0, 1, V - 1]
    for g in (0, 7):
        x["pd"][:, g][..., few] = V - 1; x["m"][:, g][..., few] = A - 1
    x["lb"][:, 7][..., few] = A - 1; x["h"][:, 7, 15][..., few] = 1; x["h"][:, 0, 15][..., few] = 0
    a = A - 1
    for _ in range(T):
        a = (4 * a + A - 1) & (A - 1); x["w"][:, 7, 15, a] = 2
    return pack(x)
def setup_inputs_corners(rng):
    x = parts(rng)
    x["sn"][0::2, 1::2] = rng.choice(np.array([0, V - 1]), x["sn"][0::2, 1::2].shape); x["sn"][1::2, 0::2, N - 2] = V - 1
    for q in range(N):
        for g in range(8):
            p, l, kind = x["pd"][q, g], x["lb"][q, g], (g + q) & 7
            if kind == 0: p[:] = np.arange(V); x["M"][q, g] = 65535; x["m"][q, g] = A - 1
            if kind == 1: p[:] = 0; x["M"][q, g] = 0; x["m"][q, g] = 0
            if kind == 2: p[:] = W - 1
            if kind == 3: p[:] = V; p[B - 1, V - 1] = V - 1; x["M"][q, g, V - 1] = 0
            if kind == 4: p[1:] = p[0]; l[1:] = l[0]
            if kind == 5: p[1:] = p[0]; x["m"][q, g] = (A - 1) * rng.integers(0, 2, V)
            if kind == 6: x["t"][q, g] = 1024; x["M"][q, g] = 7
            if kind == 7: x["t"][q, g] = -1024 * (np.arange(16)[:, None] & 1); x["M"][q, g] = 65534 + rng.integers(0, 2, V); x["w"][q, g] = at_ends(rng, -2, 2, x["w"][q, g], 0.5)
    return pack(x)
def setup_inputs_calm(rng):
    x = parts(rng); u = (np.arange(8)[None, :] + np.arange(N)[:, None]) & 3
    x["M"] = u[:, :, None] + rng.integers(0, 2, (N, 8, V))
    n = (rng.random((N, 8, 1, A)) * (2 + u[:, :, None, None])).astype(np.int64)
    x["w"] = np.where(rng.random((N, 8, 16, A)) < 0.0625 * n, x["w"] * 2.0 ** -7, 2.0 ** -20 * rng.integers(-1, 2, (N, 8, 16, A)))
    x["h"] = x["h"] * np.float32(2.0 ** -10); x["t"] = (1 + rng.random((N, 8, 16, 1))).astype(np.float32)
    x["y"] = x["t"] * rng.choice(np.array([-1, 1]), (N, 8, 16, T))
    return pack(x)
def check_inputs(d):
    bad = []
    for k, lo, hi in (("mt", 0, 65535), ("mm", 0, A - 1), ("pd", 0, W - 1), ("lb", 0, A - 1), ("sn", 0, V - 1)):
        if np.min(d[k]) < lo or np.max(d[k]) > hi: bad.append("range of " + k)
    for k, hi in (("wv", 2), ("h0", 65536), ("obs", 65536), ("th", 65536)):
        v = np.abs(d[k].astype(np.float32))
        if not np.max(v) <= hi: bad.append("range of " + k)
        if not np.all((v == 0) | (v >= 2.0 ** -20)): bad.append("least size of " + k)
    return bad
def reference(h0, mt, mm, wv, obs, th, pd, lb, sn):
    h = h0.astype(np.float32).reshape(N, 8, 16, V); M = mt.astype(np.int64); m = mm.astype(np.int64)
    w = wv.astype(np.float32).reshape(N, 8, 16, A); y = obs.astype(np.float32).reshape(N, 8, 16, T); lim = th.astype(np.float32).reshape(N, 8, 16, 1)
    pl = np.stack([gentries(a) for a in pd]).astype(np.int64); ll = np.stack([gentries(a) for a in lb]).astype(np.int64)
    sl = np.stack([gentries(a) for a in sn]).astype(np.int64).reshape(N, 8, N - 1, S)
    for t in range(T):
        hw, Mw, mw = [h], [M], [m]
        for d in range(1, N):
            ix = sl[:, :, d - 1]
            hw.append(np.roll(np.take_along_axis(h, ix[:, :, None, :], 3), (d, -1), (0, 1)))
            Mw.append(np.roll(np.take_along_axis(M, ix, 2), (d, -1), (0, 1))); mw.append(np.roll(np.take_along_axis(m, ix, 2), (d, -1), (0, 1)))
        hp = np.take_along_axis(np.concatenate(hw, axis=3), pl[:, :, None, :], 3)
        Mp = np.take_along_axis(np.concatenate(Mw, axis=2), pl, 2); mp = np.take_along_axis(np.concatenate(mw, axis=2), pl, 2)
        a = (4 * mp + ll) & (A - 1)
        wa = np.take_along_axis(w, a[:, :, None, :], 3)
        e = y[..., t:t + 1] - hp * wa
        c = np.add.reduce((np.abs(e) > lim).astype(np.int64), axis=2)
        new = (Mp + c).reshape(N, 8, B, V); k = np.argmin(new, axis=2)
        pick = k * V + np.arange(V)
        M = np.min(new, axis=2); m = np.take_along_axis(a, pick, 2); p4 = pick[:, :, None, :]
        u = np.take_along_axis(e, p4, 3) * np.take_along_axis(wa, p4, 3)
        h = np.take_along_axis(hp, p4, 3) + np.float32(0.125) * u
    return {"yh": h.reshape(N, 128, V).astype(np.float32), "ymt": M.astype(np.float32), "ymm": m.astype(np.float32)}

@@ -1,0 +1,467 @@
+from concourse.bass import DstId, RemoteDMATransfer
+from concourse.mybir import AluOpType, ActivationFunctionType
+
+ALU = AluOpType
+ACT = ActivationFunctionType
+NR, NV, NS, NA, NT = 4, 1024, 256, 4096, 4
+MAGIC = 12582912.0
+
+F, B, I, U = "float32", "bfloat16", "int32", "uint16"
+SCRATCH = {
+    "wav": ("sbuf", [128, 2 * NA], B),
+    "g2": ("sbuf", [128, 4096], B), "wb": ("sbuf", [128, 4096], B), "prod": ("sbuf", [128, 4096], F),
+    "ab": ("sbuf", [128, 4096], F), "cmp": ("sbuf", [128, 4096], B), "sg": ("sbuf", [128, 4096], B),
+    "ep": ("sbuf", [128, 1024], F), "tb": ("sbuf", [128, 1024], F), "hout": ("sbuf", [128, 1024], F),
+    "hg": ("sbuf", [128, 768], F),
+    "tin": ("sbuf", [128, 64, 32], B),
+    "raw": ("sbuf", [128, 2, 4, 64], I), "prm": ("sbuf", [128, 2, 64, 4], I),
+    "snr": ("sbuf", [128, 2, 48], I), "snq": ("sbuf", [128, 3, 48], I),
+    "snh": ("sbuf", [128, 48], U), "snm": ("sbuf", [128, 48], U),
+    "pdq": ("sbuf", [128, 3, 64, 4], I), "pdh": ("sbuf", [128, 256], U), "pdm": ("sbuf", [128, 256], U),
+    "pct": ("sbuf", [128, 64, 4], F), "pc": ("sbuf", [128, 256], F),
+    "al": ("sbuf", [128, 256], U), "ai": ("sbuf", [128, 2, 256], I),
+    "ob": ("sbuf", [128, 4], F), "ob8": ("sbuf", [128, 4], F), "tht": ("sbuf", [128, 4], F), "nth": ("sbuf", [128, 4], F),
+    "mmi": ("sbuf", [128, 8, 16], I), "t2i": ("sbuf", [128, 8, 2, 16], F), "t2o": ("sbuf", [128, 8, 2, 16], F),
+    "xp": ("sbuf", [128, 2, 64], I), "ff": ("sbuf", [128, 8, 16], F), "no": ("sbuf", [128, 8, 16], F),
+    "pi": ("sbuf", [128, 4], I), "ci": ("sbuf", [128, 4], I), "cf": ("sbuf", [128, 16], F),
+    "uu": ("sbuf", [128, 144], F), "zc": ("sbuf", [128, 144], B), "zm": ("sbuf", [128, 144], B), "zp": ("sbuf", [128, 144], B),
+    "zero": ("sbuf", [128, 128], F), "ident": ("sbuf", [128, 128], F), "sh1": ("sbuf", [128, 128], F), "sh16": ("sbuf", [128, 128], F),
+    "zerob": ("sbuf", [128, 128], B), "shd1": ("sbuf", [128, 128], B), "shd": ("sbuf", [128, 128], B),
+    "kc": ("sbuf", [128, 256], F), "rst": ("sbuf", [128, 256], F), "bs0": ("sbuf", [128, 64], I), "bs": ("sbuf", [128, 64], I),
+    "rr": ("sbuf", [128, 256], F), "dd": ("sbuf", [128, 256], F), "d1": ("sbuf", [128, 256], F), "ss": ("sbuf", [128, 256], F),
+    "xx": ("sbuf", [128, 64, 2], I), "dg": ("sbuf", [128, 64, 4], I),
+    "lq": ("sbuf", [128, 3, 64], I), "lu": ("sbuf", [128, 128], U),
+    "pay0": ("psum", [128, 512], F), "pay1": ("psum", [128, 512], F), "key0": ("psum", [128, 512], F), "key1": ("psum", [128, 512], F),
+    "key2": ("psum", [128, 512], F), "dsh": ("psum", [128, 512], F), "hs0": ("psum", [128, 512], F), "hs1": ("psum", [128, 512], F),
+}
+for _t in range(NT):
+    SCRATCH["hw%d" % _t] = ("sbuf", [128, 1792], F)
+    SCRATCH["mw%d" % _t] = ("sbuf", [128, 2816], B)
+    SCRATCH["hsn%d" % _t] = ("sbuf", [128, 768], F)
+    SCRATCH["msn%d" % _t] = ("sbuf", [128, 768], B)
+
+NDMA = 24
+SEMAPHORES = ["qv", "qs", "qp", "qg", "sent"] + ["dm%d" % k for k in range(NDMA)] + \
+             ["am%d" % t for t in range(NT)] + ["ah%d" % t for t in range(NT)]
+
+PARAM = {
+    "parts": [[64, 64], [64, 64]],
+    "p2": ["V", "V", "V", "SS"],
+    "upd": 32, "mfirst": True,
+    "cyc": 1.04, "gat": 1.6, "pe": 0.6, "fix": 70.0, "lat": 90.0,
+    "seed": 1, "iters": 3000, "w": {}, "pick": {},
+    "lat_m": 4500.0, "lat_h": 3500.0, "gap_h": 2000.0,
+}
+
+
+def plan(g, core, T, topo, P):
+    rank = T.rank_of(core)
+    ops, lastw, readers, bankuse = [], {}, {}, {}
+    cyc, gat, fix = P["cyc"], P["gat"], P["fix"]
+    chunks, parts, pieces = [], [], []
+    for p, ws in enumerate(P["parts"]):
+        c0 = chunks[-1][1] if chunks else 0
+        qs = []
+        for wd in ws:
+            a = chunks[-1][1] if chunks else 0
+            qs.append(len(chunks)); chunks.append((a, a + wd, p))
+        parts.append((c0, chunks[-1][1], qs))
+        for b0 in range(c0 // 4, chunks[-1][1] // 4, P["upd"]):
+            pieces.append((b0, min(b0 + P["upd"], chunks[-1][1] // 4), p))
+    NP = len(parts)
+    def hk(t): return ["h%d_%d" % (t, u) for u in range(len(pieces))]
+    def mk(t): return ["mw%d_%d" % (t, p) for p in range(NP)]
+
+    def op(engs, fn, reads=(), writes=(), banks=(), cost=0.0, kind="c", after=(), done=0.0, prio=None):
+        k = len(ops)
+        deps = set(after)
+        for r in reads:
+            if r in lastw: deps.add(lastw[r])
+        for w in writes:
+            if w in lastw: deps.add(lastw[w])
+            deps.update(readers.get(w, ()))
+        for b in banks:
+            u = bankuse.setdefault(b, [engs, [], []])
+            if u[0] != engs or len(engs) > 1: u[0], u[1], u[2] = engs, [], u[1]
+            deps.update(u[2]); u[1].append(k)
+        for r in reads: readers.setdefault(r, []).append(k)
+        for w in writes:
+            lastw[w] = k; readers[w] = []
+        deps.discard(k)
+        tag = writes[0] if writes else "s" + reads[0]
+        for pre in ("mwr", "mw", "smsn", "msn", "shsn", "hsn", "hr", "h"):
+            if tag.startswith(pre) and tag[len(pre)].isdigit():
+                tag = pre + tag[len(pre) + 1:]; break
+        tag = "%s.%s.%d" % (engs, tag, cost)
+        ops.append({"tag": tag, "engs": engs, "fn": fn, "deps": deps, "cost": cost, "kind": kind, "done": done, "prio": k if prio is None else prio})
+        return k
+
+    def cv(n, f=1.0): return fix + max(64, n * f) * cyc
+    def vs(out, in0, s1, s2, o0, o1, n, r, w, banks=(), f=1.0, **kw):
+        if o1 is None: return op("V", lambda e: g.vector.tensor_scalar(out, in0, s1, None, o0), r, w, banks, cv(n, f), **kw)
+        return op("V", lambda e: g.vector.tensor_scalar(out, in0, s1, s2, o0, o1), r, w, banks, cv(n, f), **kw)
+    def vt(out, in0, in1, o, n, r, w, banks=(), f=2.0, **kw):
+        return op("V", lambda e: g.vector.tensor_tensor(out, in0, in1, o), r, w, banks, cv(n, f), **kw)
+    def vc(out, in_, n, r, w, banks=(), **kw):
+        return op("V", lambda e: g.vector.tensor_copy(out, in_), r, w, banks, cv(n), **kw)
+    def vm(out, c, n, w, f=1.0):
+        return op("V", lambda e: g.vector.memset(out, c), (), w, (), cv(n, f))
+    def copy(engs, out, in_, n, r, w, banks=(), f=1.0, **kw):
+        def fn(e):
+            return g.vector.tensor_copy(out, in_) if e == "V" else g.scalar.activation(out, in_, ACT.Copy)
+        return op(engs, fn, r, w, banks, cv(n, f), **kw)
+    def act(out, in_, func, bias, scale, n, r, w, f=1.0, **kw):
+        return op("S", lambda e: g.scalar.activation(out, in_, func, bias=bias, scale=scale), r, w, (), cv(n, f), **kw)
+    def mm(lst, cols, r, w, banks, **kw):
+        def fn(e):
+            for a in lst: ins = g.tensor.matmul(*a)
+            return ins
+        return op("P", fn, r, w, banks, 60 + cols * P["pe"], **kw)
+    def dma(q, out, in_, nbytes, r, w, **kw):
+        def fn(e): return (g.sync if e == "Y" else g.scalar).dma_start(out, in_)
+        return op(q, fn, r, w, (), 60.0, kind="d", done=2000.0 + nbytes / 150.0, **kw)
+    def gp(fn, n, r, w): return op("G", lambda e: fn(), r, w, (), 170 + 2 * n * cyc)
+
+    dma("Y", T.mmi[:, 0:4, :], T.mt[:], 32768, (), ["mt"])
+    dma("S", T.mmi[:, 4:8, :], T.mm[:], 32768, (), ["mm"])
+    dma("Y", T.snr[0:112, 1, :], T.sn[16:128, :], 24576, (), ["sn1a"])
+    dma("S", T.snr[112:128, 1, :], T.sn[0:16, :], 4096, (), ["sn1b"])
+    dma("Y", T.snr[:, 0, :], T.sn[:], 24576, (), ["sn0"])
+    dma("S", T.hw0[:, 0:NV], T.h0[:], 524288, (), hk(0))
+    dma("Y", T.raw[:, 0, :, :], T.pd[:], 131072, (), ["pd"])
+    dma("Y", T.raw[:, 1, :, :], T.lb[:], 131072, (), ["lb"])
+    dma("Y", T.ob[:], T.obs[:], 2048, (), ["ob"])
+    dma("Y", T.tht[:, 0:1], T.th[:], 512, (), ["th"])
+    dma("Y", T.wav[:, 0:NA], T.wv[:], 1500000, (), ["wv0"])
+
+    cf = T.cf
+    gp(lambda: g.iota(T.pi[:, 0:1], [[0, 1]], 0, 1), 1, (), ["pi"])
+    vm(T.zero[:], 0.0, 128, ["zero"])
+    vm(T.zerob[:], 0.0, 128, ["zerob"], 0.5)
+    vs(T.ci[:, 0:1], T.pi[:, 0:1], 15, None, ALU.bitwise_and, None, 1, ["pi"], ["ci0"])
+    vs(T.ci[:, 1:2], T.pi[:, 0:1], 4, 1, ALU.arith_shift_right, ALU.bitwise_and, 1, ["pi"], ["ci1"])
+    vc(cf[:, 0:2], T.ci[:, 0:2], 2, ["ci0", "ci1"], ["cf"])
+    vs(cf[:, 2:3], cf[:, 1:2], -2048.0, 2048.0, ALU.mult, ALU.add, 1, ["cf"], ["c2"])
+    vs(cf[:, 3:4], cf[:, 1:2], 2048.0, None, ALU.mult, None, 1, ["cf"], ["c3"])
+    gp(lambda: g.affine_select(T.shd1[:], T.zerob[:], [[-32, 4], [16, 2], [-1, 16]], ALU.not_equal, 1.0, -32, 1), 128, ["zerob"], ["shd1"])
+    gp(lambda: g.affine_select(T.shd[:], T.shd1[:], [[-32, 4], [16, 2], [-1, 16]], ALU.not_equal, 1.0, 96, 1), 128, ["shd1"], ["shd"])
+    gp(lambda: g.affine_select(T.sh1[:], T.zero[:], [[-1, 128]], ALU.not_equal, 1.0, -16, 1), 128, ["zero"], ["sh1"])
+    gp(lambda: g.affine_select(T.sh16[:], T.sh1[:], [[-1, 128]], ALU.not_equal, 1.0, 112, 1), 128, ["sh1"], ["sh16"])
+    gp(lambda: g.affine_select(T.ident[:], T.zero[:], [[-1, 128]], ALU.not_equal, 1.0, 0, 1), 128, ["zero"], ["ident"])
+    gp(lambda: g.iota(T.uu[:], [[1, 144]], 0, -1, allow_small_or_imprecise_dtypes=True), 144, (), ["uu"])
+    gp(lambda: g.iota(T.kc[:], [[0, 64], [16384, 4]], 0, 0, allow_small_or_imprecise_dtypes=True), 256, (), ["kc"])
+    gp(lambda: g.iota(T.bs0[:], [[64, 64]], 0, 0), 64, (), ["bs0"])
+    vm(T.tin[:], 0.0, 2048, ["tin%s%d" % (x, p) for x in "AB" for p in range(NP)], 0.5)
+    vs(cf[:, 4:5], cf[:, 1:2], 16.0, None, ALU.mult, None, 1, ["cf"], ["c4"])
+    vs(cf[:, 5:6], cf[:, 1:2], -16.0, 16.0, ALU.mult, ALU.add, 1, ["cf"], ["c5"])
+    vs(cf[:, 12:13], cf[:, 1:2], -1.0, 1.0, ALU.mult, ALU.add, 1, ["cf"], ["c12"])
+    vs(cf[:, 6:7], cf[:, 0:1], -1.0, 15.0, ALU.mult, ALU.add, 1, ["cf"], ["c6"])
+    for j, wgt in enumerate((2.0 ** 21, 2.0 ** 29, 4.0, 1024.0)):
+        vs(cf[:, 7 + j:8 + j], cf[:, 0:1], float(j), wgt, ALU.is_equal, ALU.mult, 1, ["cf"], ["w%d" % j])
+    vt(cf[:, 13:14], cf[:, 7:8], cf[:, 8:9], ALU.add, 1, ["w0", "w1"], ["wm"])
+    vt(cf[:, 14:15], cf[:, 9:10], cf[:, 10:11], ALU.add, 1, ["w2", "w3"], ["wp"])
+
+    def spread(ps, t):
+        c0, c1 = parts[ps[0]][0], parts[ps[-1]][1]
+        bs = slice(c0 // 4, c1 // 4)
+        def ks(name): return [name + str(p) for p in ps]
+        vc(T.tin[:, bs, 0:4], T.dg[:, bs, :], c1 - c0, ks("dg0") + ks("dg1") + ks("dg2") + ks("dg3"), ks("tinA"))
+        mm([(T.dsh[:, c0:c1], T.shd[:], T.tin[:, bs, 0:4], True, True)], c1 - c0, ["shd"] + ks("tinA"), ks("dsh"), ["dsh"])
+        copy("SV", T.tin[:, bs, 16:20], T.dsh[:, c0:c1], c1 - c0, ks("dsh"), ks("tinB"), ["dsh"])
+        op("V", lambda e: g.vector.transpose(T["mw%d" % t][:, 8 * c0:8 * c1], T.tin[:, bs, :]),
+           ks("tinA") + ks("tinB"), ks("mw%d_" % t), (), cv(8 * (c1 - c0), 0.5))
+
+    peers = [T.cores[(rank + d) % NR] for d in range(1, NR)]
+
+    def show_m(t):
+        win = T["mw%d" % t][:, 0:2048]
+        r = mk(t) + ["snm"]
+        copy("VS", T["msn%d" % t][:, 0:384], win.indirect(T.snm[:, 0:24]), 384, r, ["msn%da" % t], f=gat)
+        copy("SV", T["msn%d" % t][:, 384:768], win.indirect(T.snm[:, 24:48]), 384, r, ["msn%db" % t], f=gat)
+        def fn(e):
+            trs = []
+            for d, (a, b) in enumerate(((0, 2), (4, 8), (2, 4))):
+                en = topo.engines(core, peers[d])
+                rid, pid, _ = topo.addr(peers[d])
+                trs.append(RemoteDMATransfer(dst_ids=[DstId(rid=rid, pnc=pid)], dma_engine_mask=sum(1 << x for x in en[a:b]),
+                                             remote_sem=T.sem["am%d" % t], src=T["msn%d" % t][:, 256 * d:256 * d + 256],
+                                             dst=T["mw%d" % t][:, 2048 + 256 * d:2048 + 256 * d + 256]))
+            g.remote_dma_fused(trs, local_sem=T.sem.sent)
+            return 8
+        s = op("G", fn, ["msn%da" % t, "msn%db" % t], (), (), 300.0, kind="r")
+        op("", ("am%d" % t, 8), (), ["mwr%d" % t], (), 0.0, kind="a", after=[s], done=P["lat_m"] + (2000.0 if t == 0 else 0.0))
+        return s
+
+    def show_h(t, first):
+        s = first
+        for d in range(NR - 1):
+            cs = slice(256 * d, 256 * d + 256)
+            bank = "hs%d" % (d % 2)
+            ps = T[bank][:, 256 * (d // 2):256 * (d // 2) + 256]
+            copy("SV", T.hg[:, cs], T["hw%d" % t][:, 0:NV].indirect(T.snh[:, 16 * d:16 * d + 16]), 256, hk(t) + ["snh"], ["hg%d" % d], f=gat)
+            mm([(ps, T.sh16[:], T.hg[:, cs], True, True)], 1024, ["sh16", "hg%d" % d], ["hs%d" % d], [bank])
+            copy("VS", T["hsn%d" % t][:, cs], ps, 256, ["hs%d" % d], ["hsn%d_%d" % (t, d)], [bank])
+            def fn(e, d=d, cs=cs):
+                rid, pid, _ = topo.addr(peers[d])
+                g.remote_dma(T["hw%d" % t][:, NV + 256 * d:NV + 256 * d + 256], T["hsn%d" % t][:, cs], T.sem["ah%d" % t], T.sem.sent,
+                             pid, rid, topo.mask(core, peers[d]))
+                return len(topo.engines(core, peers[d]))
+            s = op("G", fn, ["hsn%d_%d" % (t, d)], (), (), 300.0, kind="r", after=[s] if d or t == 0 or P["mfirst"] else [])
+        n = sum(len(topo.engines(p, core)) for p in peers)
+        op("", ("ah%d" % t, n), (), ["hr%d" % t], (), 0.0, kind="a", after=[s], done=P["lat_h"] + P["gap_h"])
+
+    for x in range(2):
+        vs(T.t2i[:, :, x, :], T.mmi[:], cf[:, 2 + x:3 + x], None, ALU.mult, None, 128, ["mt", "mm", "c2", "c3"], ["t2i%d" % x])
+    op("V", lambda e: g.vector.transpose(T.t2o[:], T.t2i[:]), ["t2i0", "t2i1"], ["t2o"], (), cv(256))
+    for b in range(4):
+        vt(T.xp[:, :, b::4], T.t2o[:, b::4, 0, :], T.t2o[:, b::4, 1, :], ALU.add, 32, ["t2o"], ["xp%d" % b])
+    xr = ["xp%d" % b for b in range(4)]
+    def allp(name): return [name + str(p) for p in range(NP)]
+    vs(T.dg[:, :, 0], T.xp[:, 0, :], 11, 255, ALU.arith_shift_right, ALU.bitwise_and, 64, xr, allp("dg0"))
+    vs(T.dg[:, :, 1], T.xp[:, 0, :], 19, None, ALU.arith_shift_right, None, 64, xr, allp("dg1"))
+    vs(T.dg[:, :, 2], T.xp[:, 1, :], 11, 255, ALU.arith_shift_right, ALU.bitwise_and, 64, xr, allp("dg2"))
+    vs(T.dg[:, :, 3], T.xp[:, 1, :], 19, 3, ALU.arith_shift_right, ALU.bitwise_and, 64, xr, allp("dg3"))
+    vs(T.snq[:, 0, :], T.snr[:, 1, :], 2032, None, ALU.bitwise_and, None, 48, ["sn1a", "sn1b"], ["snq0"])
+    vt(T.snq[:, 1, :], T.snq[:, 0, :], T.snr[:, 1, :], ALU.add, 48, ["snq0", "sn1a", "sn1b"], ["snq1"])
+    vs(T.snm[:], T.snq[:, 1, :], cf[:, 5:6], None, ALU.add, None, 48, ["snq1", "c5"], ["snm"])
+    spread(list(range(NP)), 0)
+    first = show_m(0)
+    vc(T.snh[:], T.snr[:, 0, :], 48, ["sn0"], ["snh"])
+    show_h(0, first)
+
+    for k in range(4):
+        vc(T.prm[:, :, :, k], T.raw[:, :, k, :], 128, ["pd", "lb"], ["prm%d" % k])
+    pr = ["prm%d" % k for k in range(4)]
+    vs(T.pdq[:, 0, :, :], T.prm[:, 0, :, :], 2032, None, ALU.bitwise_and, None, 256, pr, ["pdq0"])
+    vs(T.pdq[:, 1, :, :], T.pdq[:, 0, :, :], cf[:, 4:5], 1024.0, ALU.add, ALU.min, 256, ["pdq0", "c4"], ["pdq1"])
+    vt(T.pdq[:, 2, :, :], T.pdq[:, 1, :, :], T.prm[:, 0, :, :], ALU.add, 256, ["pdq1"] + pr, ["pdq2"])
+    vc(T.pdm[:], T.pdq[:, 2, :, :], 256, ["pdq2"], ["pdm"])
+    vs(T.pct[:], T.prm[:, 0, :, :], 1.0 / 2048, 0.5625, ALU.mult, ALU.add, 256, pr, ["pct"])
+    vt(T.pc[:], T.pct[:], T.prm[:, 1, :, :], ALU.add, 256, ["pct"] + pr, ["pc"])
+    vc(T.pdh[:], T.prm[:, 0, :, :], 256, pr, ["pdh"])
+    vs(T.zp[:], T.uu[:], cf[:, 6:7], cf[:, 14:15], ALU.is_equal, ALU.mult, 144, ["uu", "c6", "wp"], ["zp"])
+    vs(T.zm[:], T.uu[:], cf[:, 6:7], cf[:, 13:14], ALU.is_equal, ALU.mult, 144, ["uu", "c6", "wm"], ["zm"])
+    vs(T.zc[:], T.uu[:], cf[:, 6:7], 2.0 ** 21, ALU.is_equal, ALU.mult, 144, ["uu", "c6"], ["zc"])
+    vm(T.rst[:], 0.0, 256, ["rst"])
+    vm(T.rst[:, 0::4], 1e20, 64, ["rst"])
+    vs(T.bs[:], T.bs0[:], cf[:, 0:1], None, ALU.add, None, 64, ["bs0", "cf"], ["bs"])
+    vs(T.ob8[:], T.ob[:], 0.125, None, ALU.mult, None, 4, ["ob"], ["ob8"])
+    vs(T.nth[:, 0:1], T.tht[:, 0:1], -1.0, None, ALU.mult, None, 1, ["th"], ["nth"])
+
+    def extract(z, src, out, q, stop):
+        c0, c1, _ = chunks[q]
+        return [(out[:, c0:c1], z[:, 15 - i:143 - i], src[:, 16 * c0 + i:16 * c1:16], False, stop and i == 15) for i in range(16)]
+
+    for t in range(NT):
+        hw, mw = T["hw%d" % t], T["mw%d" % t]
+        last = t == NT - 1
+        for p, (c0, c1, qs) in enumerate(parts):
+            mm([(T["key%d" % p][:, c0:c1], T.ident[:], T.kc[:, c0:c1], True, False)], 4 * (c1 - c0), ["ident", "kc"],
+               ["kc%d" % p] + ["key%d" % q for q in qs], ["key%d" % p])
+        for q, (c0, c1, p) in enumerate(chunks):
+            n, k, bank, cs = 16 * (c1 - c0), str(q), "pay%d" % (q % 2), slice(c0, c1)
+            pay, wd = T[bank][:, cs], c1 - c0
+            copy("SV", T.g2[:, 16 * c0:16 * c1], mw[:].indirect(T.pdm[:, cs]), n, mk(t) + ["mwr%d" % t, "pdm"], ["g2" + k], f=gat)
+            mm([(pay, T.ident[:], T.pc[:, cs], True, False)], 4 * max(wd, 64), ["ident", "pc"], ["payc" + k, "pay" + k, "grp" + bank], [bank])
+            mm(extract(T.zp, T.g2, T[bank], q, True), 16 * max(wd, 64), ["zp", "g2" + k], ["pay" + k, "grp" + bank], [bank])
+            if t == 0:
+                vs(T.ai[:, 0, cs], pay, MAGIC, MAGIC + 1, ALU.add, ALU.subtract, wd, ["pay" + k], ["ai0" + k], [bank])
+                vs(T.ai[:, 1, cs], T.ai[:, 0, cs], NA - 1, None, ALU.bitwise_and, None, wd, ["ai0" + k], ["ai1" + k])
+                vc(T.al[:, cs], T.ai[:, 1, cs], wd, ["ai1" + k], ["al" + k])
+            else:
+                vs(T.al[:, cs], pay, MAGIC, MAGIC + 1, ALU.add, ALU.subtract, wd, ["pay" + k], ["al" + k], [bank])
+            mm(extract(T.zm, T.g2, T["key%d" % p], q, False), 16 * max(wd, 64), ["zm", "g2" + k], ["keym" + k, "key" + k], ["key%d" % p])
+            win = T.wav[:, 0:NA] if t == 0 else T.wav[:]
+            copy("SV", T.wb[:, 16 * c0:16 * c1], win.indirect(T.al[:, cs]), n, ["wv0", "al" + k] + ([] if t == 0 else ["wv1"]), ["wb" + k], f=gat)
+        if t == 0:
+            dma("Y", T.wav[:, NA:2 * NA], T.wv[:], 1048576, ["hr0"], ["wv1"])
+        for q, (c0, c1, p) in enumerate(chunks):
+            n, k, js = 16 * (c1 - c0), str(q), slice(16 * c0, 16 * c1)
+            vt(T.prod[:, js], hw[:].indirect(T.pdh[:, c0:c1]), T.wb[:, js], ALU.mult, n, hk(t) + ["hr%d" % t, "pdh", "wb" + k], ["prod" + k], f=gat)
+            act(T.ab[:, js], T.prod[:, js], ACT.Abs, T.ob[:, t:t + 1], -1.0, n, ["prod" + k, "ob"], ["ab" + k])
+            mode = P["p2"][q]
+            if mode == "V":
+                vs(T.cmp[:, js], T.ab[:, js], T.tht[:, 0:1], None, ALU.is_gt, None, n, ["ab" + k, "th"], ["cmp" + k])
+            else:
+                act(T.sg[:, js], T.ab[:, js], ACT.Sign, T.nth[:, 0:1], 1.0, n, ["ab" + k, "nth"], ["sg" + k])
+                if mode == "S":
+                    vs(T.cmp[:, js], T.sg[:, js], 0.0, None, ALU.max, None, n, ["sg" + k], ["cmp" + k], f=0.5)
+                else:
+                    act(T.cmp[:, js], T.sg[:, js], ACT.Relu, 0.0, 1.0, n, ["sg" + k], ["cmp" + k])
+            c0, c1, qs = parts[p]
+            kk = ["key%d" % j for j in qs]
+            mm(extract(T.zc, T.cmp, T["key%d" % p], q, q == qs[-1]), 16 * max(n // 16, 64), ["zc", "cmp" + k] + (kk if q == qs[-1] else []),
+               ["key" + k], ["key%d" % p])
+            if q != qs[-1]: continue
+            wd, nb, b0 = c1 - c0, (c1 - c0) // 4, c0 // 4
+            bs, cs, s = slice(b0, b0 + nb), slice(c0, c1), str(p)
+            key = T["key" + s][:, cs]
+            op("V", lambda e, cs=cs, key=key: g.vector.tensor_tensor_scan(T.rr[:, cs], T.rst[:, cs], key, 0.0, ALU.add, ALU.min),
+               kk + ["rst"], ["rr" + s], ["key" + s], cv(wd))
+            vt(T.dd[:, cs], key, T.rr[:, cs], ALU.subtract, wd, kk + ["rr" + s], ["dd" + s], ["key" + s], f=1.0)
+            vs(T.xx[:, bs, 0], T.rr[:, c0 + 3:c1:4], 2.0 ** -10, None, ALU.mult, None, nb, ["rr" + s], ["x0" + s])
+            for j in qs:
+                a0, a1, _ = chunks[j]
+                vt(T.d1[:, a0:a1], T["pay%d" % (j % 2)][:, a0:a1], T.dd[:, a0:a1], ALU.subtract, a1 - a0, ["pay%d" % j, "dd" + s], ["d1%d" % j],
+                   ["pay%d" % (j % 2)], f=1.0)
+            vs(T.lq[:, 0, bs], T.xx[:, bs, 0], 48, None, ALU.bitwise_and, None, nb, ["x0" + s], ["lq0" + s])
+            op("V", lambda e, cs=cs: g.vector.tensor_tensor_scan(T.ss[:, cs], T.dd[:, cs], T.d1[:, cs], 0.0, ALU.min, ALU.max),
+               ["dd" + s] + ["d1%d" % j for j in qs], ["ss" + s], (), cv(wd))
+            vt(T.lq[:, 1, bs], T.lq[:, 0, bs], T.bs[:, 0:nb], ALU.add, nb, ["lq0" + s, "bs"], ["lq1" + s])
+            vs(T.xx[:, bs, 1], T.ss[:, c0 + 3:c1:4], 2048.0, -1152.0, ALU.mult, ALU.add, nb, ["ss" + s], ["x1" + s])
+            if not last:
+                vs(T.dg[:, bs, 1], T.xx[:, bs, 0], 19, None, ALU.arith_shift_right, None, nb, ["x0" + s], ["dg1" + s])
+                vs(T.dg[:, bs, 0::2], T.xx[:, bs, :], 11, 255, ALU.arith_shift_right, ALU.bitwise_and, 2 * nb, ["x0" + s, "x1" + s], ["dg0" + s, "dg2" + s])
+                vs(T.dg[:, bs, 3], T.xx[:, bs, 1], 19, 3, ALU.arith_shift_right, ALU.bitwise_and, nb, ["x1" + s], ["dg3" + s])
+            vs(T.lq[:, 2, bs], T.xx[:, bs, 1], 2047, None, ALU.bitwise_and, None, nb, ["x1" + s], ["lq2" + s])
+            vc(T.lu[:, 2 * b0:2 * b0 + 2 * nb], T.lq[:, 1:3, bs], 2 * nb, ["lq1" + s, "lq2" + s], ["lu" + s])
+            if not last:
+                spread([p], t + 1)
+                if p == NP - 1: first = show_m(t + 1)
+            ws = slice(16 * c0, 16 * c1)
+            for u, (u0, u1, pu) in enumerate(pieces):
+                if pu != p: continue
+                pick, pds = T.lu[:, b0 + u0:b0 + u1], T.lu[:, b0 + nb + u0:b0 + nb + u1]
+                vsl, m, su = slice(16 * u0, 16 * u1), 16 * (u1 - u0), str(u)
+                act(T.ep[:, vsl], T.prod[:, ws].indirect(pick), ACT.Identity, T.ob8[:, t:t + 1], -0.125, m,
+                    ["prod%d" % j for j in qs] + ["lu" + s, "ob8"], ["ep" + su], f=gat)
+                vt(T.tb[:, vsl], T.wb[:, ws].indirect(pick), T.ep[:, vsl], ALU.mult, m, ["wb%d" % j for j in qs] + ["lu" + s, "ep" + su],
+                   ["tb" + su], f=gat)
+                dst = T.hout if last else T["hw%d" % (t + 1)]
+                vt(dst[:, vsl], hw[:].indirect(pds), T.tb[:, vsl], ALU.add, m, hk(t) + ["hr%d" % t, "lu" + s, "tb" + su], [hk(t + 1)[u]], f=gat)
+                if last:
+                    dma("Y", T.yh[:, vsl], T.hout[:, vsl], 512 * m, [hk(t + 1)[u]], ["yh" + su])
+        if not last:
+            show_h(t + 1, first)
+
+    xr = allp("x0") + allp("x1")
+    vs(T.xp[:, 0, :], T.xx[:, :, 0], 11, None, ALU.arith_shift_right, None, 64, xr, ["xp0", "xp1"])
+    vs(T.xp[:, 1, :], T.xx[:, :, 1], 11, NA - 1, ALU.arith_shift_right, ALU.bitwise_and, 64, xr, ["xp2", "xp3"])
+    for b in range(4):
+        vc(T.ff[:, b::4, :], T.xp[:, :, b::4], 32, ["xp0", "xp2"], ["ff%d" % b])
+    fr = ["ff%d" % b for b in range(4)]
+    vs(T.t2i[:, :, 0, :], T.ff[:], cf[:, 12:13], None, ALU.mult, None, 128, fr + ["c12"], ["t2i0"])
+    vs(T.t2i[:, :, 1, :], T.ff[:], cf[:, 1:2], None, ALU.mult, None, 128, fr + ["cf"], ["t2i1"])
+    op("V", lambda e: g.vector.transpose(T.t2o[:], T.t2i[:]), ["t2i0", "t2i1"], ["t2o"], (), cv(256))
+    vt(T.no[:], T.t2o[:, :, 0, :], T.t2o[:, :, 1, :], ALU.add, 128, ["t2o"], ["no"])
+    dma("Y", T.ymt[:], T.no[:, 0:4, :], 32768, ["no"], ["ymt"])
+    dma("S", T.ymm[:], T.no[:, 4:8, :], 32768, ["no"], ["ymm"])
+    return ops
+
+
+def schedule(ops, P):
+    n, lat = len(ops), P["lat"]
+    succ = [[] for _ in ops]
+    for k, o in enumerate(ops):
+        for d in o["deps"]: succ[d].append(k)
+    rnd = [P["seed"]]
+    def rand():
+        rnd[0] = (rnd[0] * 6364136223846793005 + 1442695040888963407) % (1 << 64)
+        return (rnd[0] >> 33) / float(1 << 31)
+
+    lev = [0.0] * n
+    for k in range(n - 1, -1, -1):
+        lev[k] = ops[k]["cost"] + ops[k]["done"] + lat + max([lev[j] for j in succ[k]] + [0.0])
+
+    def run(w, pick):
+        busy = {e: [] for e in "VSPGY"}
+        fin, start, eng = [0.0] * n, [0.0] * n, [""] * n
+        pri = [lev[k] + w.get(o["tag"], 0.0) for k, o in enumerate(ops)]
+        missing = [len(o["deps"]) for o in ops]
+        cand = [k for k in range(n) if not missing[k]]
+        while cand:
+            k = max(cand, key=lambda j: pri[j]); cand.remove(k)
+            for j in succ[k]:
+                missing[j] -= 1
+                if not missing[j]: cand.append(j)
+            o = ops[k]; c = o["cost"]
+            ready = max([fin[d] + lat for d in o["deps"]] + [0.0])
+            best = (ready, "", 0)
+            for e in (pick.get(o["tag"]) or o["engs"]):
+                st, bz = ready, busy[e]
+                i = len(bz)
+                while i > 0 and bz[i - 1][1] > ready: i -= 1
+                while i < len(bz) and bz[i][0] < st + c:
+                    st = max(st, bz[i][1]); i += 1
+                if best[1] == "" or st < best[0]: best = (st, e, i)
+            st, e, i = best
+            if e: busy[e].insert(i, (st, st + c))
+            start[k], eng[k], fin[k] = st, e, st + c + o["done"]
+        return max(fin), start, eng, fin
+
+    free = sorted(set(o["tag"] for o in ops if len(o["engs"]) > 1))
+    tags = sorted(set(o["tag"] for o in ops))
+    big = sorted(set(o["tag"] for o in ops if o["cost"] > 400))
+    w, pick = dict(P["w"]), dict(P["pick"])
+    cur = best = run(w, pick)
+    keep = (w, pick)
+    for it in range(P["iters"]):
+        w2, p2 = dict(w), dict(pick)
+        for _j in range(1 + int(3 * rand())):
+            x = rand()
+            if free and x < 0.25:
+                p2[free[int(rand() * len(free))]] = "VS"[int(2 * rand())]
+            else:
+                pool = big if x < 0.75 else tags
+                w2[pool[int(rand() * len(pool))]] = float(int(16000 * (rand() - 0.5) * (0.2 + rand())))
+        r = run(w2, p2)
+        if r[0] <= cur[0] + 600.0 * (1 - it / P["iters"]) * rand():
+            cur, w, pick = r, w2, p2
+            if r[0] < best[0]: best, keep = r, (w2, p2)
+    P["found"] = keep
+    for k, o in enumerate(ops):
+        o["start"], o["eng"], o["fin"] = best[1][k], best[2][k], best[3][k]
+    return sorted(range(n), key=lambda k: (best[1][k], k))
+
+
+def emit(g, T, ops, seq):
+    queue = {"V": g.vector, "S": g.scalar, "P": g.tensor, "G": g, "Y": g.sync}
+    qsem = {"V": "qv", "S": "qs", "P": "qp", "G": "qg"}
+    pos, cnt, ndma = {}, {e: 0 for e in queue}, 0
+    known = {e: {} for e in queue}
+    snap, waits, need = {}, {}, set()
+    for k in seq:
+        o = ops[k]
+        if o["kind"] == "a":
+            pos[k] = (o["fn"][0], 1); snap[k] = {o["fn"][0]: 1}; continue
+        e = o["eng"]; kn = known[e]; w = []
+        for d in sorted(o["deps"], key=lambda d: -ops[d]["fin"]):
+            od = ops[d]
+            if od["kind"] == "r" or (e == "P" and od["eng"] == "P"): continue
+            s, v = pos[d]
+            if kn.get(s, 0) >= v: continue
+            w.append(d); need.add(d)
+            for s2, v2 in snap[d].items():
+                if kn.get(s2, 0) < v2: kn[s2] = v2
+        waits[k] = w
+        if o["kind"] == "d":
+            pos[k] = ("dm%d" % ndma, 1); ndma += 1
+        elif o["kind"] == "c":
+            cnt[e] += 1; pos[k] = (qsem[e], cnt[e])
+        if o["kind"] != "r":
+            snap[k] = dict(kn); snap[k][pos[k][0]] = pos[k][1]
+    val, tot, waited = {}, {}, {}
+    for k in seq:
+        o = ops[k]
+        if o["kind"] == "a":
+            val[k] = o["fn"]; tot[o["fn"][0]] = o["fn"][1]; continue
+        e = o["eng"]
+        for d in waits[k]:
+            s, v = val[d]
+            queue[e].wait_ge(T.sem[s], v); waited[s] = max(waited.get(s, 0), v)
+        ins = o["fn"](e)
+        if o["kind"] == "r":
+            tot["sent"] = tot.get("sent", 0) + ins
+        elif o["kind"] == "d":
+            s = pos[k][0]; ins.then_inc(T.sem[s], 16); val[k] = (s, 16); tot[s] = 16
+        elif k in need:
+            s = qsem[e]; tot[s] = tot.get(s, 0) + 1; ins.then_inc(T.sem[s], 1); val[k] = (s, tot[s])
+    for s, v in tot.items():
+        if waited.get(s, 0) < v: g.wait_ge(T.sem[s], v)
+
+
+def rank_program(g, core, T, topo):
+    if T.rank_of(core) is None:
+        return
+    ops = plan(g, core, T, topo, PARAM)
+    emit(g, T, ops, schedule(ops, PARAM))

@@ -22,7 +22,7 @@ SCRATCH = {
     "al": ("sbuf", [128, 256], U), "ai": ("sbuf", [128, 2, 256], I),
     "ob": ("sbuf", [128, 4], F), "ob8": ("sbuf", [128, 4], F), "tht": ("sbuf", [128, 4], F), "nth": ("sbuf", [128, 4], F),
     "mmi": ("sbuf", [128, 8, 16], I), "t2i": ("sbuf", [128, 8, 2, 16], F), "t2o": ("sbuf", [128, 8, 2, 16], F),
-    "xp": ("sbuf", [128, 2, 64], I), "ff": ("sbuf", [128, 8, 16], F), "no": ("sbuf", [128, 8, 16], F),
+    "xp": ("sbuf", [128, 2, 64], I), "ff": ("sbuf", [128, 2, 64], F), "no": ("sbuf", [128, 8, 16], F),
     "pi": ("sbuf", [128, 4], I), "ci": ("sbuf", [128, 4], I), "cf": ("sbuf", [128, 16], F),
     "uu": ("sbuf", [128, 144], F), "zc": ("sbuf", [128, 144], B), "zm": ("sbuf", [128, 144], B), "zp": ("sbuf", [128, 144], B),
     "zero": ("sbuf", [128, 128], F), "ident": ("sbuf", [128, 128], F), "sh1": ("sbuf", [128, 128], F), "sh16": ("sbuf", [128, 128], F),
@@ -45,9 +45,11 @@ SEMAPHORES = ["qv", "qs", "qp", "qg", "sent"] + ["dm%d" % k for k in range(NDMA)
              ["am%d" % t for t in range(NT)] + ["ah%d" % t for t in range(NT)]
 
 PARAM = {
-    "parts": [[64, 64], [64, 64]],
-    "p2": ["V", "V", "V", "SS"],
-    "upd": 32, "mfirst": True,
+    "parts": [[64, 64, 64, 64]],
+    "p2": ["V", "SS", "V", "V"],
+    "upd": 32, "mfirst": True, "bank": [0, 0, 1, 1],
+    "order": [0,1,2,3,4,5,6,7,8,9,10,27,11,13,15,19,14,16,12,20,17,29,18,32,21,39,38,24,28,40,23,35,44,41,26,43,42,25,49,47,46,48,45,60,22,52,77,53,31,50,54,34,51,55,56,57,76,61,58,75,74,65,59,62,91,37,78,82,66,63,79,69,64,80,67,70,68,84,93,81,71,33,83,72,73,85,111,95,110,94,87,102,112,126,96,113,114,119,115,97,98,103,118,99,104,36,101,117,120,105,106,107,127,109,121,92,122,123,86,128,131,116,108,125,124,136,100,132,140,133,137,129,141,138,130,134,30,139,142,135,88,89,90,143,144,145,147,148,146,199,150,187,153,152,155,154,158,149,159,156,151,160,157,161,166,169,167,163,170,162,168,164,165,171,176,172,180,173,177,174,175,181,178,186,179,182,198,183,184,192,188,204,200,185,189,201,205,191,193,203,194,206,208,195,207,197,210,202,196,190,209,214,211,219,215,223,216,220,212,224,221,213,217,225,222,218,226,227,228,230,268,231,233,282,229,270,235,236,237,238,241,232,242,239,234,243,240,244,249,252,250,246,253,245,251,247,248,254,255,259,256,263,260,257,258,264,261,269,262,265,281,266,267,275,271,287,283,272,284,288,274,276,286,277,289,279,278,290,280,293,285,291,273,292,297,294,302,298,306,299,303,295,307,304,296,300,308,305,301,309,310,311,313,351,314,312,316,365,353,319,318,320,321,324,315,325,322,317,326,323,327,332,335,333,329,336,328,334,330,331,337,346,338,342,339,343,340,341,347,344,352,345,348,364,349,350,358,354,370,366,355,367,371,357,359,369,360,372,362,361,373,363,376,368,374,356,375,380,377,385,381,389,382,386,378,390,387,379,383,391,388,384,392,393,394,395,396,397,399,398,401,400,402,403,412,404,413,414,408,405,417,409,418,415,416,419,421,422,420,406,410,407,423,411,424,425,426],
+    "eng": "YSYSYSYYYYYGVVVVVVVGGGGGGGGVVVVVVVVVVVVVVVVVVVVVVVVVVPSVVSG VSPSGSPSGSPSG VVVVVVVVVVVVVVVVVVVPVPPVVVPVSPPVVVPSSPPVVVPSSPPVVVPSYVSVPVSSSPVSVPVSVPVVVVVVVVVVVVVVVPSVSSG SVVSVVSPSGVPSGVPSG PVPPVPVVPPVPSSPPVPSSPPVPSVSVPVSSSPVSVPVSVPVVVVVVVVVVVVVVVPSVSSG SVVSVVSPVGSPSGSPSG PVPPVPVVPPVPSSPPVPSSPPVPSVSVPVSSSPVSVPVSVPVVVVVVVVVVVVVVVPSVSSG SVVSVVSPSGSPSGVPSG PVPPVPVVPPVPSSPPVPSSPPVPSVSVPVSSSPVSVPVSVPVVVVVVVVVVVSVVYSVVYVVVSSSSSSSSVVYS",
     "cyc": 1.04, "gat": 1.6, "pe": 0.6, "fix": 70.0, "lat": 90.0,
     "seed": 1, "iters": 3000, "w": {}, "pick": {},
     "lat_m": 4500.0, "lat_h": 3500.0, "gap_h": 2000.0,
@@ -189,7 +191,7 @@ def plan(g, core, T, topo, P):
             g.remote_dma_fused(trs, local_sem=T.sem.sent)
             return 8
         s = op("G", fn, ["msn%da" % t, "msn%db" % t], (), (), 300.0, kind="r")
-        op("", ("am%d" % t, 8), (), ["mwr%d" % t], (), 0.0, kind="a", after=[s], done=P["lat_m"] + (2000.0 if t == 0 else 0.0))
+        op("", ("am%d" % t, 8), (), ["mwr%d" % t], (), 0.0, kind="a", after=[s], done=P["lat_m"] + (P.get("lat_0", 2000.0) if t == 0 else 0.0))
         return s
 
     def show_h(t, first):
@@ -259,7 +261,7 @@ def plan(g, core, T, topo, P):
             mm([(T["key%d" % p][:, c0:c1], T.ident[:], T.kc[:, c0:c1], True, False)], 4 * (c1 - c0), ["ident", "kc"],
                ["kc%d" % p] + ["key%d" % q for q in qs], ["key%d" % p])
         for q, (c0, c1, p) in enumerate(chunks):
-            n, k, bank, cs = 16 * (c1 - c0), str(q), "pay%d" % (q % 2), slice(c0, c1)
+            n, k, bank, cs = 16 * (c1 - c0), str(q), "pay%d" % P["bank"][q], slice(c0, c1)
             pay, wd = T[bank][:, cs], c1 - c0
             copy("SV", T.g2[:, 16 * c0:16 * c1], mw[:].indirect(T.pdm[:, cs]), n, mk(t) + ["mwr%d" % t, "pdm"], ["g2" + k], f=gat)
             mm([(pay, T.ident[:], T.pc[:, cs], True, False)], 4 * max(wd, 64), ["ident", "pc"], ["payc" + k, "pay" + k, "grp" + bank], [bank])
@@ -300,10 +302,14 @@ def plan(g, core, T, topo, P):
                kk + ["rst"], ["rr" + s], ["key" + s], cv(wd))
             vt(T.dd[:, cs], key, T.rr[:, cs], ALU.subtract, wd, kk + ["rr" + s], ["dd" + s], ["key" + s], f=1.0)
             vs(T.xx[:, bs, 0], T.rr[:, c0 + 3:c1:4], 2.0 ** -10, None, ALU.mult, None, nb, ["rr" + s], ["x0" + s])
+            runs = []
             for j in qs:
-                a0, a1, _ = chunks[j]
-                vt(T.d1[:, a0:a1], T["pay%d" % (j % 2)][:, a0:a1], T.dd[:, a0:a1], ALU.subtract, a1 - a0, ["pay%d" % j, "dd" + s], ["d1%d" % j],
-                   ["pay%d" % (j % 2)], f=1.0)
+                if runs and P["bank"][runs[-1][0]] == P["bank"][j]: runs[-1].append(j)
+                else: runs.append([j])
+            for r in runs:
+                a0, a1, bank = chunks[r[0]][0], chunks[r[-1]][1], "pay%d" % P["bank"][r[0]]
+                vt(T.d1[:, a0:a1], T[bank][:, a0:a1], T.dd[:, a0:a1], ALU.subtract, a1 - a0, ["pay%d" % j for j in r] + ["dd" + s],
+                   ["d1%d" % j for j in r], [bank], f=1.0)
             vs(T.lq[:, 0, bs], T.xx[:, bs, 0], 48, None, ALU.bitwise_and, None, nb, ["x0" + s], ["lq0" + s])
             op("V", lambda e, cs=cs: g.vector.tensor_tensor_scan(T.ss[:, cs], T.dd[:, cs], T.d1[:, cs], 0.0, ALU.min, ALU.max),
                ["dd" + s] + ["d1%d" % j for j in qs], ["ss" + s], (), cv(wd))
@@ -337,12 +343,14 @@ def plan(g, core, T, topo, P):
     xr = allp("x0") + allp("x1")
     vs(T.xp[:, 0, :], T.xx[:, :, 0], 11, None, ALU.arith_shift_right, None, 64, xr, ["xp0", "xp1"])
     vs(T.xp[:, 1, :], T.xx[:, :, 1], 11, NA - 1, ALU.arith_shift_right, ALU.bitwise_and, 64, xr, ["xp2", "xp3"])
+    vc(T.ff[:], T.xp[:], 128, ["xp0", "xp2"], ["ff"])
     for b in range(4):
-        vc(T.ff[:, b::4, :], T.xp[:, :, b::4], 32, ["xp0", "xp2"], ["ff%d" % b])
-    fr = ["ff%d" % b for b in range(4)]
-    vs(T.t2i[:, :, 0, :], T.ff[:], cf[:, 12:13], None, ALU.mult, None, 128, fr + ["c12"], ["t2i0"])
-    vs(T.t2i[:, :, 1, :], T.ff[:], cf[:, 1:2], None, ALU.mult, None, 128, fr + ["cf"], ["t2i1"])
-    op("V", lambda e: g.vector.transpose(T.t2o[:], T.t2i[:]), ["t2i0", "t2i1"], ["t2o"], (), cv(256))
+        for x, col in enumerate((cf[:, 12:13], cf[:, 1:2])):
+            def fn(e, b=b, x=x, col=col):
+                if e == "V": return g.vector.tensor_scalar(T.t2i[:, b::4, x, :], T.ff[:, :, b::4], col, None, ALU.mult)
+                return g.scalar.activation(T.t2i[:, b::4, x, :], T.ff[:, :, b::4], ACT.Identity, scale=col)
+            op("SV", fn, ["ff", "c12", "cf", "t2o"], ["tj%d%d" % (b, x)], (), cv(32))
+    op("V", lambda e: g.vector.transpose(T.t2o[:], T.t2i[:]), ["tj%d%d" % (b, x) for b in range(4) for x in range(2)], ["t2o"], (), cv(256))
     vt(T.no[:], T.t2o[:, :, 0, :], T.t2o[:, :, 1, :], ALU.add, 128, ["t2o"], ["no"])
     dma("Y", T.ymt[:], T.no[:, 0:4, :], 32768, ["no"], ["ymt"])
     dma("S", T.ymm[:], T.no[:, 4:8, :], 32768, ["no"], ["ymm"])
@@ -351,6 +359,10 @@ def plan(g, core, T, topo, P):
 
 def schedule(ops, P):
     n, lat = len(ops), P["lat"]
+    if P["order"]:
+        for i, k in enumerate(P["order"]):
+            ops[k]["eng"] = P["eng"][k].strip(); ops[k]["start"] = ops[k]["fin"] = float(i)
+        return list(P["order"])
     succ = [[] for _ in ops]
     for k, o in enumerate(ops):
         for d in o["deps"]: succ[d].append(k)

@@ -12,27 +12,28 @@ SCRATCH = {
     "g2": ("sbuf", [128, 4096], B), "wb": ("sbuf", [128, 4096], B), "prod": ("sbuf", [128, 4096], F),
     "ab": ("sbuf", [128, 4096], F), "cmp": ("sbuf", [128, 4096], B), "sg": ("sbuf", [128, 4096], B),
     "ep": ("sbuf", [128, 1024], F), "tb": ("sbuf", [128, 1024], F), "hout": ("sbuf", [128, 1024], F),
-    "hg": ("sbuf", [128, 768], F),
-    "tin": ("sbuf", [128, 64, 32], B),
+    "hmv": ("sbuf", [128, 1024], F), "wsl": ("sbuf", [128, 1024], B), "hq": ("sbuf", [128, 1024], F),
+    "tin": ("sbuf", [128, 64, 32], B), "mwq": ("sbuf", [128, 2048], B),
     "raw": ("sbuf", [128, 2, 4, 64], I), "prm": ("sbuf", [128, 2, 64, 4], I),
-    "snr": ("sbuf", [128, 2, 48], I), "snq": ("sbuf", [128, 3, 48], I),
-    "snh": ("sbuf", [128, 48], U), "snm": ("sbuf", [128, 48], U),
+    "snr": ("sbuf", [128, 2, 48], I), "snq": ("sbuf", [128, 3, 48], I), "snf": ("sbuf", [128, 2, 48], F),
+    "snh": ("sbuf", [128, 48], U), "snm": ("sbuf", [128, 48], U), "sn0": ("sbuf", [128, 48], U),
     "pdq": ("sbuf", [128, 3, 64, 4], I), "pdh": ("sbuf", [128, 256], U), "pdm": ("sbuf", [128, 256], U),
     "pct": ("sbuf", [128, 64, 4], F), "pc": ("sbuf", [128, 256], F),
     "al": ("sbuf", [128, 256], U), "ai": ("sbuf", [128, 2, 256], I),
-    "ob": ("sbuf", [128, 4], F), "ob8": ("sbuf", [128, 4], F), "tht": ("sbuf", [128, 4], F), "nth": ("sbuf", [128, 4], F),
-    "mmi": ("sbuf", [128, 8, 16], I), "t2i": ("sbuf", [128, 8, 2, 16], F), "t2o": ("sbuf", [128, 8, 2, 16], F),
+    "ob": ("sbuf", [128, 4], F), "ob8": ("sbuf", [128, 4], F), "tht": ("sbuf", [128, 4], F),
+    "mmi": ("sbuf", [128, 2, 64], I), "t2i": ("sbuf", [128, 8, 2, 16], F), "t2o": ("sbuf", [128, 8, 2, 16], F),
     "xp": ("sbuf", [128, 2, 64], I), "ff": ("sbuf", [128, 2, 64], F), "no": ("sbuf", [128, 8, 16], F),
     "pi": ("sbuf", [128, 4], I), "ci": ("sbuf", [128, 4], I), "cf": ("sbuf", [128, 16], F),
     "uu": ("sbuf", [128, 144], F), "zc": ("sbuf", [128, 144], B), "zm": ("sbuf", [128, 144], B), "zp": ("sbuf", [128, 144], B),
-    "zero": ("sbuf", [128, 128], F), "ident": ("sbuf", [128, 128], F), "sh1": ("sbuf", [128, 128], F), "sh16": ("sbuf", [128, 128], F),
-    "zerob": ("sbuf", [128, 128], B), "shd1": ("sbuf", [128, 128], B), "shd": ("sbuf", [128, 128], B),
-    "kc": ("sbuf", [128, 256], F), "rst": ("sbuf", [128, 256], F), "bs0": ("sbuf", [128, 64], I), "bs": ("sbuf", [128, 64], I),
+    "zero": ("sbuf", [128, 128], B), "idb": ("sbuf", [128, 128], B), "ident": ("sbuf", [128, 128], F), "id14": ("sbuf", [128, 128], B),
+    "sh1": ("sbuf", [128, 128], B), "shb": ("sbuf", [128, 128], B), "shf": ("sbuf", [128, 128], F),
+    "kc": ("sbuf", [128, 256], B), "cen": ("sbuf", [128, 256], B), "rst": ("sbuf", [128, 256], F),
+    "nat0": ("sbuf", [128, 64], I), "nat": ("sbuf", [128, 64], U),
     "rr": ("sbuf", [128, 256], F), "dd": ("sbuf", [128, 256], F), "d1": ("sbuf", [128, 256], F), "ss": ("sbuf", [128, 256], F),
     "xx": ("sbuf", [128, 64, 2], I), "dg": ("sbuf", [128, 64, 4], I),
-    "lq": ("sbuf", [128, 3, 64], I), "lu": ("sbuf", [128, 128], U),
-    "pay0": ("psum", [128, 512], F), "pay1": ("psum", [128, 512], F), "key0": ("psum", [128, 512], F), "key1": ("psum", [128, 512], F),
-    "key2": ("psum", [128, 512], F), "dsh": ("psum", [128, 512], F), "hs0": ("psum", [128, 512], F), "hs1": ("psum", [128, 512], F),
+    "lq": ("sbuf", [128, 2, 64], I), "lu": ("sbuf", [128, 128], U),
+    "pay": ("psum", [128, 4, 512], F), "key": ("psum", [128, 512], F),
+    "hs": ("psum", [128, 2, 512], F), "hs2": ("psum", [128, 512], F),
 }
 for _t in range(NT):
     SCRATCH["hw%d" % _t] = ("sbuf", [128, 1792], F)
@@ -40,41 +41,75 @@ for _t in range(NT):
     SCRATCH["hsn%d" % _t] = ("sbuf", [128, 768], F)
     SCRATCH["msn%d" % _t] = ("sbuf", [128, 768], B)
 
-NDMA = 24
+NDMA = 40
 SEMAPHORES = ["qv", "qs", "qp", "qg", "sent"] + ["dm%d" % k for k in range(NDMA)] + \
-             ["am%d" % t for t in range(NT)] + ["ah%d" % t for t in range(NT)]
+             ["am%d" % t for t in range(NT)] + ["ah%d" % t for t in range(NT)] + ["fw%d" % t for t in range(NT)]
 
-PARAM = {
-    "parts": [[64, 64, 64, 64]],
-    "p2": ["V", "SS", "V", "V"],
-    "upd": 32, "mfirst": True, "bank": [0, 0, 1, 1],
-    "order": [0,1,2,3,4,5,6,7,8,9,10,27,11,13,15,19,14,16,12,20,17,29,18,32,21,39,38,24,28,40,23,35,44,41,26,43,42,25,49,47,46,48,45,60,22,52,77,53,31,50,54,34,51,55,56,57,76,61,58,75,74,65,59,62,91,37,78,82,66,63,79,69,64,80,67,70,68,84,93,81,71,33,83,72,73,85,111,95,110,94,87,102,112,126,96,113,114,119,115,97,98,103,118,99,104,36,101,117,120,105,106,107,127,109,121,92,122,123,86,128,131,116,108,125,124,136,100,132,140,133,137,129,141,138,130,134,30,139,142,135,88,89,90,143,144,145,147,148,146,199,150,187,153,152,155,154,158,149,159,156,151,160,157,161,166,169,167,163,170,162,168,164,165,171,176,172,180,173,177,174,175,181,178,186,179,182,198,183,184,192,188,204,200,185,189,201,205,191,193,203,194,206,208,195,207,197,210,202,196,190,209,214,211,219,215,223,216,220,212,224,221,213,217,225,222,218,226,227,228,230,268,231,233,282,229,270,235,236,237,238,241,232,242,239,234,243,240,244,249,252,250,246,253,245,251,247,248,254,255,259,256,263,260,257,258,264,261,269,262,265,281,266,267,275,271,287,283,272,284,288,274,276,286,277,289,279,278,290,280,293,285,291,273,292,297,294,302,298,306,299,303,295,307,304,296,300,308,305,301,309,310,311,313,351,314,312,316,365,353,319,318,320,321,324,315,325,322,317,326,323,327,332,335,333,329,336,328,334,330,331,337,346,338,342,339,343,340,341,347,344,352,345,348,364,349,350,358,354,370,366,355,367,371,357,359,369,360,372,362,361,373,363,376,368,374,356,375,380,377,385,381,389,382,386,378,390,387,379,383,391,388,384,392,393,394,395,396,397,399,398,401,400,402,403,412,404,413,414,408,405,417,409,418,415,416,419,421,422,420,406,410,407,423,411,424,425,426],
-    "eng": "YSYSYSYYYYYGVVVVVVVGGGGGGGGVVVVVVVVVVVVVVVVVVVVVVVVVVPSVVSG VSPSGSPSGSPSG VVVVVVVVVVVVVVVVVVVPVPPVVVPVSPPVVVPSSPPVVVPSSPPVVVPSYVSVPVSSSPVSVPVSVPVVVVVVVVVVVVVVVPSVSSG SVVSVVSPSGVPSGVPSG PVPPVPVVPPVPSSPPVPSSPPVPSVSVPVSSSPVSVPVSVPVVVVVVVVVVVVVVVPSVSSG SVVSVVSPVGSPSGSPSG PVPPVPVVPPVPSSPPVPSSPPVPSVSVPVSSSPVSVPVSVPVVVVVVVVVVVVVVVPSVSSG SVVSVVSPSGSPSGVPSG PVPPVPVVPPVPSSPPVPSSPPVPSVSVPVSSSPVSVPVSVPVVVVVVVVVVVSVVYSVVYVVVSSSSSSSSVVYS",
-    "cyc": 1.04, "gat": 1.6, "pe": 0.6, "fix": 70.0, "lat": 90.0,
-    "seed": 1, "iters": 3000, "w": {}, "pick": {},
-    "lat_m": 4500.0, "lat_h": 3500.0, "gap_h": 2000.0,
+CHUNKS = [64, 64, 64, 32, 32]
+ON_SCALAR = [[3], [3]]
+PIECES = [24, 24, 16]
+LAST_PIECES = [24, 24, 16]
+MOVE_BY_DMA = []
+H_ON_SCALAR = []
+VIA_PSUM = [[1, 1, 0], [2, 2, 0]]
+CUT, CLOSE = 192, "2"
+SPLIT = ["rr", "d1", "pk"]
+SPLIT_LAST = ["rr", "d1", "pk", "pd"]
+CALLS_M = [[0, 1], [2]]
+CALLS_H = [[0, 2], [1]]
+HANDED = []
+
+ORDER = {
+    "V": ["zero tin0 ci1 ci0 cf dMh dMl dmh dml sq tinA snh su cpb sv w1 sn0 tr w0 ms0 c32 w3 prm0 rst c6 prm2 prm1 nat w2 wm rs4 "
+          "prm3 zm pq0 pdh pq1 sm0 c12 sm1 pct pq2 wp snm zp cen zc pc pdm",
+          "dig0 dig2 ai0 ai3 ai1 am0 am1 am3 al0 ai2 al3 al1 wg3 ai4 am2 am4 al2 al4 pr3 pr0 pr1 pr2 cm0 pr4 cm1 cm2 cm4 "
+          "rr dd x0 d1 pk1 rrb pk ddb x0b d1b pk1b ss ssb pkb x1 dMh dlo dmh pd1 tinA tb0 pdl tb2 tr hn0 tb1 hn1 hn2 hc1 hg0",
+          "dig0 al0 dig2 al1 dig4 al2 al3 pr0 pr1 al4 pr2 pr3 pr4 cm0 cm1 cm2 cm4 rr x0 dd pk1 pk d1 rrb ss ddb ws0 x1 d1b pd1 ssb "
+          "x0b x1b xM pdl xm pk1b pd1b tb1 fm pdlb pkb tb0 fM hn0 hn1 tb2 hn2 t2 no"],
+    "S": ["shf tinB ident id14 ms1 ms2 hc1 hc0 own hg0 hg1 hg2 nth ob8",
+          "dig1 dig3 dig4 wg0 wg1 wg2 ab0 ab3 wg4 ab1 ab2 ab4 sg3 cm3 ws0 ep0 ep2 tinB ws1 ep1 ms0 ms1 ms2 hc0 hc2 hg2 hg1",
+          "dig3 dig1 wg0 wg1 wg2 wg3 wg4 ab0 ab1 ab4 ab2 ab3 sg3 cm3 ep1 ws1 ep0 hp0 hp1 ep2 tj0 tj1 tj2 tj3 tj4 tj5 tj6 tj7"],
+    "P": ["sh hs0 hs1",
+          "pc2 pc0 pc1 pc3 kc xa0 xa1 xa3 xa2 pc4 xa4 kcb xm1 xm3 xm4 xm0 xm2 xc0 xc1 xc2 xc3 xc4 wp0 sh wp1 hs0 hs1 hs2",
+          "pc0 pc1 pc3 pc2 kc xa0 xa1 xa2 xa3 pc4 xm1 xa4 kcb xm0 xm4 xm3 xm2 xc0 xc1 xc2 xc3 xc4 wp1 wp0"],
 }
 
 
-def plan(g, core, T, topo, P):
-    rank = T.rank_of(core)
-    ops, lastw, readers, bankuse = [], {}, {}, {}
-    cyc, gat, fix = P["cyc"], P["gat"], P["fix"]
-    chunks, parts, pieces = [], [], []
-    for p, ws in enumerate(P["parts"]):
-        c0 = chunks[-1][1] if chunks else 0
-        qs = []
-        for wd in ws:
-            a = chunks[-1][1] if chunks else 0
-            qs.append(len(chunks)); chunks.append((a, a + wd, p))
-        parts.append((c0, chunks[-1][1], qs))
-        for b0 in range(c0 // 4, chunks[-1][1] // 4, P["upd"]):
-            pieces.append((b0, min(b0 + P["upd"], chunks[-1][1] // 4), p))
-    NP = len(parts)
-    def hk(t): return ["h%d_%d" % (t, u) for u in range(len(pieces))]
-    def mk(t): return ["mw%d_%d" % (t, p) for p in range(NP)]
+def helper(T, topo, rank, d):
+    core, peer = T.cores[rank], T.cores[(rank + d + 1) % NR]
+    able = [c for c in topo.cores_of(core) if topo.die(c) != topo.die(core) and topo.may_write(c, peer)]
+    return able[HANDED.index(d) % len(able)]
 
-    def op(engs, fn, reads=(), writes=(), banks=(), cost=0.0, kind="c", after=(), done=0.0, prio=None):
+
+def on_chip_engines(T, topo, rank, d):
+    core, peer = T.cores[rank], T.cores[(rank + d + 1) % NR]
+    return [e for e in topo.engines(core, helper(T, topo, rank, d)) if e not in topo.engines(core, peer)]
+
+
+def hand_on(g, core, T, topo, rank, d):
+    peer = T.cores[(rank + d + 1) % NR]
+    rid, pid, _ = topo.addr(peer)
+    call = [[x for x in ds if x in HANDED] for ds in CALLS_H if d in ds][0]
+    for t in range(NT):
+        g.wait_ge(T.sem["fw%d" % t], len(on_chip_engines(T, topo, rank, d)) // len(call))
+        g.remote_dma(T["hw%d" % t][:, NV + 256 * d:NV + 256 * d + 256], T["hsn%d" % t][:, 256 * d:256 * d + 256], T.sem["ah%d" % t], T.sem.sent,
+                     pid, rid, topo.mask(core, peer))
+    g.wait_ge(T.sem.sent, NT * len(topo.engines(core, peer)))
+
+
+def plan(g, core, T, topo):
+    rank = T.rank_of(core)
+    ops, lastw, readers, bankuse, now = [], {}, {}, {}, [-1]
+    ends = [sum(CHUNKS[:q]) for q in range(len(CHUNKS) + 1)]
+    chunks = list(zip(ends, ends[1:]))
+    def cuts(ws): return [(sum(ws[:u]), sum(ws[:u + 1])) for u in range(len(ws))]
+    def hk(t): return ["h%d_%d" % (t, u) for u in range(len(PIECES))] if t else ["h0"]
+    def within(name, c0, c1): return [name + str(q) for q, (a, b) in enumerate(chunks) if c0 <= a < c1]
+    def spans(name, split):
+        def k(sfx): return lambda *names: [nm + x for nm in names for x in sfx]
+        return [(0, CUT, "", k([""])), (CUT, 256, "b", k(["b"]))] if name in split else [(0, 256, "", k(["", "b"]))]
+
+    def op(name, engs, fn, reads=(), writes=(), banks=(), kind="c", after=()):
         k = len(ops)
         deps = set(after)
         for r in reads:
@@ -90,345 +125,327 @@ def plan(g, core, T, topo, P):
         for w in writes:
             lastw[w] = k; readers[w] = []
         deps.discard(k)
-        tag = writes[0] if writes else "s" + reads[0]
-        for pre in ("mwr", "mw", "smsn", "msn", "shsn", "hsn", "hr", "h"):
-            if tag.startswith(pre) and tag[len(pre)].isdigit():
-                tag = pre + tag[len(pre) + 1:]; break
-        tag = "%s.%s.%d" % (engs, tag, cost)
-        ops.append({"tag": tag, "engs": engs, "fn": fn, "deps": deps, "cost": cost, "kind": kind, "done": done, "prio": k if prio is None else prio})
+        ops.append({"name": (now[0], name), "engs": engs, "fn": fn, "deps": deps, "kind": kind})
         return k
 
-    def cv(n, f=1.0): return fix + max(64, n * f) * cyc
-    def vs(out, in0, s1, s2, o0, o1, n, r, w, banks=(), f=1.0, **kw):
-        if o1 is None: return op("V", lambda e: g.vector.tensor_scalar(out, in0, s1, None, o0), r, w, banks, cv(n, f), **kw)
-        return op("V", lambda e: g.vector.tensor_scalar(out, in0, s1, s2, o0, o1), r, w, banks, cv(n, f), **kw)
-    def vt(out, in0, in1, o, n, r, w, banks=(), f=2.0, **kw):
-        return op("V", lambda e: g.vector.tensor_tensor(out, in0, in1, o), r, w, banks, cv(n, f), **kw)
-    def vc(out, in_, n, r, w, banks=(), **kw):
-        return op("V", lambda e: g.vector.tensor_copy(out, in_), r, w, banks, cv(n), **kw)
-    def vm(out, c, n, w, f=1.0):
-        return op("V", lambda e: g.vector.memset(out, c), (), w, (), cv(n, f))
-    def copy(engs, out, in_, n, r, w, banks=(), f=1.0, **kw):
+    def vs(name, out, in0, s1, s2, o0, o1, r, w=None, banks=()):
+        w = [name] if w is None else w
+        if o1 is None: return op(name, "V", lambda e: g.vector.tensor_scalar(out, in0, s1, None, o0), r, w, banks)
+        return op(name, "V", lambda e: g.vector.tensor_scalar(out, in0, s1, s2, o0, o1), r, w, banks)
+    def vt(name, out, in0, in1, o, r, w=None, banks=()):
+        return op(name, "V", lambda e: g.vector.tensor_tensor(out, in0, in1, o), r, [name] if w is None else w, banks)
+    def vc(name, out, in_, r, w=None):
+        return op(name, "V", lambda e: g.vector.tensor_copy(out, in_), r, [name] if w is None else w)
+    def vm(name, out, c, w=None):
+        return op(name, "V", lambda e: g.vector.memset(out, c), (), [name] if w is None else w)
+    def copy(name, out, in_, r, w=None, banks=()):
         def fn(e):
             return g.vector.tensor_copy(out, in_) if e == "V" else g.scalar.activation(out, in_, ACT.Copy)
-        return op(engs, fn, r, w, banks, cv(n, f), **kw)
-    def act(out, in_, func, bias, scale, n, r, w, f=1.0, **kw):
-        return op("S", lambda e: g.scalar.activation(out, in_, func, bias=bias, scale=scale), r, w, (), cv(n, f), **kw)
-    def mm(lst, cols, r, w, banks, **kw):
+        return op(name, "VS", fn, r, [name] if w is None else w, banks)
+    def act(name, out, in_, func, bias, scale, r, w=None):
+        return op(name, "S", lambda e: g.scalar.activation(out, in_, func, bias=bias, scale=scale), r, [name] if w is None else w)
+    def mm(name, lst, r, w, banks):
         def fn(e):
             for a in lst: ins = g.tensor.matmul(*a)
             return ins
-        return op("P", fn, r, w, banks, 60 + cols * P["pe"], **kw)
-    def dma(q, out, in_, nbytes, r, w, **kw):
+        return op(name, "P", fn, r, w, banks)
+    def dma(name, q, out, in_, r, w=None):
         def fn(e): return (g.sync if e == "Y" else g.scalar).dma_start(out, in_)
-        return op(q, fn, r, w, (), 60.0, kind="d", done=2000.0 + nbytes / 150.0, **kw)
-    def gp(fn, n, r, w): return op("G", lambda e: fn(), r, w, (), 170 + 2 * n * cyc)
+        return op(name, q, fn, r, [name] if w is None else w, (), kind="d")
+    def gp(name, fn, r): return op(name, "G", lambda e: fn(), r, [name])
 
-    dma("Y", T.mmi[:, 0:4, :], T.mt[:], 32768, (), ["mt"])
-    dma("S", T.mmi[:, 4:8, :], T.mm[:], 32768, (), ["mm"])
-    dma("Y", T.snr[0:112, 1, :], T.sn[16:128, :], 24576, (), ["sn1a"])
-    dma("S", T.snr[112:128, 1, :], T.sn[0:16, :], 4096, (), ["sn1b"])
-    dma("Y", T.snr[:, 0, :], T.sn[:], 24576, (), ["sn0"])
-    dma("S", T.hw0[:, 0:NV], T.h0[:], 524288, (), hk(0))
-    dma("Y", T.raw[:, 0, :, :], T.pd[:], 131072, (), ["pd"])
-    dma("Y", T.raw[:, 1, :, :], T.lb[:], 131072, (), ["lb"])
-    dma("Y", T.ob[:], T.obs[:], 2048, (), ["ob"])
-    dma("Y", T.tht[:, 0:1], T.th[:], 512, (), ["th"])
-    dma("Y", T.wav[:, 0:NA], T.wv[:], 1500000, (), ["wv0"])
+    dma("mt", "Y", T.mmi[:, 0, :], T.mt[:], ())
+    dma("mm", "S", T.mmi[:, 1, :], T.mm[:], ())
+    dma("sn1a", "Y", T.snr[0:112, 1, :], T.sn[16:128, :], ())
+    dma("sn1b", "S", T.snr[112:128, 1, :], T.sn[0:16, :], ())
+    dma("h0", "S", T.hw0[:, 0:NV], T.h0[:], ())
+    dma("pd", "Y", T.raw[:, 0, :, :], T.pd[:], ())
+    dma("lb", "Y", T.raw[:, 1, :, :], T.lb[:], ())
+    dma("ob", "Y", T.ob[:], T.obs[:], ())
+    dma("th", "Y", T.tht[:, 0:1], T.th[:], ())
+    dma("wv0", "Y", T.wav[:, 0:NA], T.wv[:], ())
 
     cf = T.cf
-    gp(lambda: g.iota(T.pi[:, 0:1], [[0, 1]], 0, 1), 1, (), ["pi"])
-    vm(T.zero[:], 0.0, 128, ["zero"])
-    vm(T.zerob[:], 0.0, 128, ["zerob"], 0.5)
-    vs(T.ci[:, 0:1], T.pi[:, 0:1], 15, None, ALU.bitwise_and, None, 1, ["pi"], ["ci0"])
-    vs(T.ci[:, 1:2], T.pi[:, 0:1], 4, 1, ALU.arith_shift_right, ALU.bitwise_and, 1, ["pi"], ["ci1"])
-    vc(cf[:, 0:2], T.ci[:, 0:2], 2, ["ci0", "ci1"], ["cf"])
-    vs(cf[:, 2:3], cf[:, 1:2], -2048.0, 2048.0, ALU.mult, ALU.add, 1, ["cf"], ["c2"])
-    vs(cf[:, 3:4], cf[:, 1:2], 2048.0, None, ALU.mult, None, 1, ["cf"], ["c3"])
-    gp(lambda: g.affine_select(T.shd1[:], T.zerob[:], [[-32, 4], [16, 2], [-1, 16]], ALU.not_equal, 1.0, -32, 1), 128, ["zerob"], ["shd1"])
-    gp(lambda: g.affine_select(T.shd[:], T.shd1[:], [[-32, 4], [16, 2], [-1, 16]], ALU.not_equal, 1.0, 96, 1), 128, ["shd1"], ["shd"])
-    gp(lambda: g.affine_select(T.sh1[:], T.zero[:], [[-1, 128]], ALU.not_equal, 1.0, -16, 1), 128, ["zero"], ["sh1"])
-    gp(lambda: g.affine_select(T.sh16[:], T.sh1[:], [[-1, 128]], ALU.not_equal, 1.0, 112, 1), 128, ["sh1"], ["sh16"])
-    gp(lambda: g.affine_select(T.ident[:], T.zero[:], [[-1, 128]], ALU.not_equal, 1.0, 0, 1), 128, ["zero"], ["ident"])
-    gp(lambda: g.iota(T.uu[:], [[1, 144]], 0, -1, allow_small_or_imprecise_dtypes=True), 144, (), ["uu"])
-    gp(lambda: g.iota(T.kc[:], [[0, 64], [16384, 4]], 0, 0, allow_small_or_imprecise_dtypes=True), 256, (), ["kc"])
-    gp(lambda: g.iota(T.bs0[:], [[64, 64]], 0, 0), 64, (), ["bs0"])
-    vm(T.tin[:], 0.0, 2048, ["tin%s%d" % (x, p) for x in "AB" for p in range(NP)], 0.5)
-    vs(cf[:, 4:5], cf[:, 1:2], 16.0, None, ALU.mult, None, 1, ["cf"], ["c4"])
-    vs(cf[:, 5:6], cf[:, 1:2], -16.0, 16.0, ALU.mult, ALU.add, 1, ["cf"], ["c5"])
-    vs(cf[:, 12:13], cf[:, 1:2], -1.0, 1.0, ALU.mult, ALU.add, 1, ["cf"], ["c12"])
-    vs(cf[:, 6:7], cf[:, 0:1], -1.0, 15.0, ALU.mult, ALU.add, 1, ["cf"], ["c6"])
-    for j, wgt in enumerate((2.0 ** 21, 2.0 ** 29, 4.0, 1024.0)):
-        vs(cf[:, 7 + j:8 + j], cf[:, 0:1], float(j), wgt, ALU.is_equal, ALU.mult, 1, ["cf"], ["w%d" % j])
-    vt(cf[:, 13:14], cf[:, 7:8], cf[:, 8:9], ALU.add, 1, ["w0", "w1"], ["wm"])
-    vt(cf[:, 14:15], cf[:, 9:10], cf[:, 10:11], ALU.add, 1, ["w2", "w3"], ["wp"])
-
-    def spread(ps, t):
-        c0, c1 = parts[ps[0]][0], parts[ps[-1]][1]
-        bs = slice(c0 // 4, c1 // 4)
-        def ks(name): return [name + str(p) for p in ps]
-        vc(T.tin[:, bs, 0:4], T.dg[:, bs, :], c1 - c0, ks("dg0") + ks("dg1") + ks("dg2") + ks("dg3"), ks("tinA"))
-        mm([(T.dsh[:, c0:c1], T.shd[:], T.tin[:, bs, 0:4], True, True)], c1 - c0, ["shd"] + ks("tinA"), ks("dsh"), ["dsh"])
-        copy("SV", T.tin[:, bs, 16:20], T.dsh[:, c0:c1], c1 - c0, ks("dsh"), ks("tinB"), ["dsh"])
-        op("V", lambda e: g.vector.transpose(T["mw%d" % t][:, 8 * c0:8 * c1], T.tin[:, bs, :]),
-           ks("tinA") + ks("tinB"), ks("mw%d_" % t), (), cv(8 * (c1 - c0), 0.5))
+    gp("pi", lambda: g.iota(T.pi[:, 0:1], [[0, 1]], 0, 1), ())
+    vm("zero", T.zero[:], 0.0)
+    vm("tin0", T.tin[:], 0.0, ["tinA", "tinB", "tinAb", "tinBb"])
+    gp("sh1", lambda: g.affine_select(T.sh1[:], T.zero[:], [[-1, 128]], ALU.not_equal, 1.0, -16, 1), ["zero"])
+    gp("shb", lambda: g.affine_select(T.shb[:], T.sh1[:], [[-1, 128]], ALU.not_equal, 1.0, 112, 1), ["sh1"])
+    gp("nat0", lambda: g.iota(T.nat0[:], [[1, 16], [512, 4]], 0, 0), ())
+    gp("idb", lambda: g.affine_select(T.idb[:], T.zero[:], [[-1, 128]], ALU.not_equal, 1.0, 0, 1), ["zero"])
+    gp("uu", lambda: g.iota(T.uu[:], [[1, 144]], 0, -1, allow_small_or_imprecise_dtypes=True), ())
+    gp("kcol", lambda: g.iota(T.kc[:], [[1, 256]], 0, 0, allow_small_or_imprecise_dtypes=True), ())
+    vs("ci0", T.ci[:, 0:1], T.pi[:, 0:1], 15, None, ALU.bitwise_and, None, ["pi"])
+    vs("ci1", T.ci[:, 1:2], T.pi[:, 0:1], 4, 1, ALU.arith_shift_right, ALU.bitwise_and, ["pi"])
+    vc("cf", cf[:, 0:2], T.ci[:, 0:2], ["ci0", "ci1"])
+    vs("c32", cf[:, 2:3], cf[:, 0:1], 32.0, None, ALU.mult, None, ["cf"])
+    vs("cpb", cf[:, 3:4], cf[:, 0:1], -16.0 * CUT, None, ALU.add, None, ["cf"])
+    vs("c12", cf[:, 12:13], cf[:, 1:2], -1.0, 1.0, ALU.mult, ALU.add, ["cf"])
+    vs("c6", cf[:, 6:7], cf[:, 0:1], -1.0, 15.0, ALU.mult, ALU.add, ["cf"])
+    for j, wgt in enumerate((2.0 ** 22, 2.0 ** 30, 4.0, 1024.0)):
+        vs("w%d" % j, cf[:, 7 + j:8 + j], cf[:, 0:1], float(j), wgt, ALU.is_equal, ALU.mult, ["cf"])
+    vt("wm", cf[:, 13:14], cf[:, 7:8], cf[:, 8:9], ALU.add, ["w0", "w1"])
+    vt("wp", cf[:, 14:15], cf[:, 9:10], cf[:, 10:11], ALU.add, ["w2", "w3"])
+    copy("shf", T.shf[:], T.shb[:], ["shb"])
+    copy("ident", T.ident[:], T.idb[:], ["idb"])
+    act("id14", T.id14[:], T.idb[:], ACT.Identity, 0.0, 2.0 ** 14, ["idb"])
+    vs("nat", T.nat[:], T.nat0[:], cf[:, 2:3], None, ALU.add, None, ["nat0", "c32"])
 
     peers = [T.cores[(rank + d) % NR] for d in range(1, NR)]
 
-    def show_m(t):
-        win = T["mw%d" % t][:, 0:2048]
-        r = mk(t) + ["snm"]
-        copy("VS", T["msn%d" % t][:, 0:384], win.indirect(T.snm[:, 0:24]), 384, r, ["msn%da" % t], f=gat)
-        copy("SV", T["msn%d" % t][:, 384:768], win.indirect(T.snm[:, 24:48]), 384, r, ["msn%db" % t], f=gat)
-        def fn(e):
-            trs = []
-            for d, (a, b) in enumerate(((0, 2), (4, 8), (2, 4))):
-                en = topo.engines(core, peers[d])
-                rid, pid, _ = topo.addr(peers[d])
-                trs.append(RemoteDMATransfer(dst_ids=[DstId(rid=rid, pnc=pid)], dma_engine_mask=sum(1 << x for x in en[a:b]),
-                                             remote_sem=T.sem["am%d" % t], src=T["msn%d" % t][:, 256 * d:256 * d + 256],
-                                             dst=T["mw%d" % t][:, 2048 + 256 * d:2048 + 256 * d + 256]))
-            g.remote_dma_fused(trs, local_sem=T.sem.sent)
-            return 8
-        s = op("G", fn, ["msn%da" % t, "msn%db" % t], (), (), 300.0, kind="r")
-        op("", ("am%d" % t, 8), (), ["mwr%d" % t], (), 0.0, kind="a", after=[s], done=P["lat_m"] + (P.get("lat_0", 2000.0) if t == 0 else 0.0))
-        return s
-
-    def show_h(t, first):
-        s = first
+    def show_m(t, split):
+        own = T.mwq if t == 0 else T["mw%d" % t]
+        lst, base = (T.sn0, NV) if t == 0 else (T.snm, 2 * NV)
+        for c0, c1, s, k in spans("tr", split):
+            bs = slice(c0 // 4, c1 // 4)
+            vc("tinA" + s, T.tin[:, bs, 0:4], T.dg[:, bs, :], k("dg0", "dg1", "dg2", "dg3"), k("tinA"))
+            mm("sh" + s, [(T.hs2[:, c0:c1], T.shb[:], T.tin[:, bs, 0:4], True, True)], ["shb"] + k("tinA"), k("dsh"), ["hs2"])
+            copy("tinB" + s, T.tin[:, bs, 16:20], T.hs2[:, c0:c1], k("dsh"), k("tinB"), ["hs2"])
+            op("tr" + s, "V", lambda e, c0=c0, c1=c1, bs=bs: g.vector.transpose(own[:, 8 * c0:8 * c1], T.tin[:, bs, :]), k("tinA", "tinB"), k("tr%d" % t))
+        r = ["tr%d" % t, "tr%db" % t, "sn0" if t == 0 else "snm"]
         for d in range(NR - 1):
-            cs = slice(256 * d, 256 * d + 256)
-            bank = "hs%d" % (d % 2)
-            ps = T[bank][:, 256 * (d // 2):256 * (d // 2) + 256]
-            copy("SV", T.hg[:, cs], T["hw%d" % t][:, 0:NV].indirect(T.snh[:, 16 * d:16 * d + 16]), 256, hk(t) + ["snh"], ["hg%d" % d], f=gat)
-            mm([(ps, T.sh16[:], T.hg[:, cs], True, True)], 1024, ["sh16", "hg%d" % d], ["hs%d" % d], [bank])
-            copy("VS", T["hsn%d" % t][:, cs], ps, 256, ["hs%d" % d], ["hsn%d_%d" % (t, d)], [bank])
-            def fn(e, d=d, cs=cs):
-                rid, pid, _ = topo.addr(peers[d])
-                g.remote_dma(T["hw%d" % t][:, NV + 256 * d:NV + 256 * d + 256], T["hsn%d" % t][:, cs], T.sem["ah%d" % t], T.sem.sent,
-                             pid, rid, topo.mask(core, peers[d]))
-                return len(topo.engines(core, peers[d]))
-            s = op("G", fn, ["hsn%d_%d" % (t, d)], (), (), 300.0, kind="r", after=[s] if d or t == 0 or P["mfirst"] else [])
-        n = sum(len(topo.engines(p, core)) for p in peers)
-        op("", ("ah%d" % t, n), (), ["hr%d" % t], (), 0.0, kind="a", after=[s], done=P["lat_h"] + P["gap_h"])
+            copy("ms%d" % d, T["msn%d" % t][:, 256 * d:256 * d + 256], own[:, 0:2048].indirect(lst[:, 16 * d:16 * d + 16]), r, ["msn%d_%d" % (t, d)])
+        send("m", CALLS_M, T["msn%d" % t], T["mw%d" % t], base, t)
+        if t == 0: copy("own", T.mw0[:, 0:NV], T.mwq[:].indirect(T.nat[:]), ["tr0", "nat"])
 
-    for x in range(2):
-        vs(T.t2i[:, :, x, :], T.mmi[:], cf[:, 2 + x:3 + x], None, ALU.mult, None, 128, ["mt", "mm", "c2", "c3"], ["t2i%d" % x])
-    op("V", lambda e: g.vector.transpose(T.t2o[:], T.t2i[:]), ["t2i0", "t2i1"], ["t2o"], (), cv(256))
-    for b in range(4):
-        vt(T.xp[:, :, b::4], T.t2o[:, b::4, 0, :], T.t2o[:, b::4, 1, :], ALU.add, 32, ["t2o"], ["xp%d" % b])
-    xr = ["xp%d" % b for b in range(4)]
-    def allp(name): return [name + str(p) for p in range(NP)]
-    vs(T.dg[:, :, 0], T.xp[:, 0, :], 11, 255, ALU.arith_shift_right, ALU.bitwise_and, 64, xr, allp("dg0"))
-    vs(T.dg[:, :, 1], T.xp[:, 0, :], 19, None, ALU.arith_shift_right, None, 64, xr, allp("dg1"))
-    vs(T.dg[:, :, 2], T.xp[:, 1, :], 11, 255, ALU.arith_shift_right, ALU.bitwise_and, 64, xr, allp("dg2"))
-    vs(T.dg[:, :, 3], T.xp[:, 1, :], 19, 3, ALU.arith_shift_right, ALU.bitwise_and, 64, xr, allp("dg3"))
-    vs(T.snq[:, 0, :], T.snr[:, 1, :], 2032, None, ALU.bitwise_and, None, 48, ["sn1a", "sn1b"], ["snq0"])
-    vt(T.snq[:, 1, :], T.snq[:, 0, :], T.snr[:, 1, :], ALU.add, 48, ["snq0", "sn1a", "sn1b"], ["snq1"])
-    vs(T.snm[:], T.snq[:, 1, :], cf[:, 5:6], None, ALU.add, None, 48, ["snq1", "c5"], ["snm"])
-    spread(list(range(NP)), 0)
-    first = show_m(0)
-    vc(T.snh[:], T.snr[:, 0, :], 48, ["sn0"], ["snh"])
-    show_h(0, first)
+    def send(x, calls, src, dst, base, t):
+        sem, n = "a%s%d" % (x, t), 0
+        for c, ds in enumerate(calls):
+            handed = [d for d in ds if x == "h" and d in HANDED]
+            direct = [d for d in ds if d not in handed]
+            def fn(e, handed=handed, direct=direct):
+                trs, used = [], 0
+                for d in direct + handed:
+                    block = src[:, 256 * d:256 * d + 256]
+                    if d in direct:
+                        to, mine = peers[d], topo.engines(core, peers[d])[direct.index(d)::len(direct)]
+                        land, arrive = dst[:, base + 256 * d:base + 256 * d + 256], sem
+                    else:
+                        to = helper(T, topo, rank, d)
+                        mine, land, arrive = on_chip_engines(T, topo, rank, d)[handed.index(d)::len(handed)], block, "fw%d" % t
+                    rid, pid, _ = topo.addr(to)
+                    trs.append(RemoteDMATransfer(dst_ids=[DstId(rid=rid, pnc=pid)], dma_engine_mask=sum(1 << i for i in mine), remote_sem=T.sem[arrive],
+                                                 src=block, dst=land))
+                    used += len(mine)
+                g.remote_dma_fused(trs, local_sem=T.sem.sent)
+                return used
+            s = op("send%s%d" % (x, c), "G", fn, ["%ssn%d_%d" % (x, t, d) for d in ds], kind="r")
+            n += sum(len(topo.engines(T.cores[(rank - d - 1) % NR], core)) // len(direct) for d in direct)
+            n += sum(len(topo.engines(helper(T, topo, (rank - d - 1) % NR, d), core)) for d in handed)
+        op("got" + x, "", (sem, n), (), ["%sr%d" % (x, t)], kind="a", after=[s])
+
+    def move(u, src, cols, name):
+        if now[0] >= 0 and u in MOVE_BY_DMA:
+            for x, (to, fro) in enumerate(((slice(0, 112), slice(16, 128)), (slice(112, 128), slice(0, 16)))):
+                k = dma("hd%d%d" % (u, x), "Y", T.hmv[to, cols], src[fro, cols], [name], ["hm%d" % u + "x" * x])
+                ops[k]["deps"].update(readers.get("snh", ()))
+            return
+        ps, hs = T.hs[:, u % 2, 0:cols.stop - cols.start], "hs%d" % (u % 2)
+        mm("hs%d" % u, [(ps, T.shf[:], src[:, cols], True, True)], ["shf", name], [hs], [hs])
+        k = copy("hc%d" % u, T.hmv[:, cols], ps, [hs], ["hm%d" % u], [hs])
+        ops[k]["deps"].update(readers.get("snh", ()))
+
+    def show_h(t, moved):
+        for d in range(NR - 1):
+            copy("hg%d" % d, T["hsn%d" % t][:, 256 * d:256 * d + 256], T.hmv[:].indirect(T.snh[:, 16 * d:16 * d + 16]), moved + ["snh"], ["hsn%d_%d" % (t, d)])
+        send("h", CALLS_H, T["hsn%d" % t], T["hw%d" % t], NV, t)
+
+    sr = ["sn1a", "sn1b"]
+    vs("sq", T.snq[:, 0, :], T.snr[:, 1, :], 6, None, ALU.arith_shift_right, None, sr)
+    vs("su", T.snf[:, 0, :], T.snq[:, 0, :], -2047.0 / 32, None, ALU.mult, None, ["sq"])
+    vt("sv", T.snf[:, 1, :], T.snf[:, 0, :], T.snr[:, 1, :], ALU.add, ["su"] + sr)
+    vs("sn0", T.sn0[:], T.snf[:, 1, :], 32.0, 16.0, ALU.mult, ALU.add, ["sv"])
+    vs("dMl", T.dg[:, :, 0], T.mmi[:, 0, :], 255, None, ALU.bitwise_and, None, ["mt"], ["dg0"])
+    vs("dMh", T.dg[:, :, 1], T.mmi[:, 0, :], 8, None, ALU.arith_shift_right, None, ["mt"], ["dg1"])
+    vs("dml", T.dg[:, :, 2], T.mmi[:, 1, :], 255, None, ALU.bitwise_and, None, ["mm"], ["dg2"])
+    vs("dmh", T.dg[:, :, 3], T.mmi[:, 1, :], 8, 3, ALU.arith_shift_right, ALU.bitwise_and, ["mm"], ["dg3"])
+    show_m(0, ())
+    vc("snh", T.snh[:], T.snr[:, 1, :], sr)
+    for u in range(2): move(u, T.hw0, slice(512 * u, 512 * u + 512), "h0")
+    show_h(0, ["hm0", "hm1"])
 
     for k in range(4):
-        vc(T.prm[:, :, :, k], T.raw[:, :, k, :], 128, ["pd", "lb"], ["prm%d" % k])
+        vc("prm%d" % k, T.prm[:, :, :, k], T.raw[:, :, k, :], ["pd", "lb"])
     pr = ["prm%d" % k for k in range(4)]
-    vs(T.pdq[:, 0, :, :], T.prm[:, 0, :, :], 2032, None, ALU.bitwise_and, None, 256, pr, ["pdq0"])
-    vs(T.pdq[:, 1, :, :], T.pdq[:, 0, :, :], cf[:, 4:5], 1024.0, ALU.add, ALU.min, 256, ["pdq0", "c4"], ["pdq1"])
-    vt(T.pdq[:, 2, :, :], T.pdq[:, 1, :, :], T.prm[:, 0, :, :], ALU.add, 256, ["pdq1"] + pr, ["pdq2"])
-    vc(T.pdm[:], T.pdq[:, 2, :, :], 256, ["pdq2"], ["pdm"])
-    vs(T.pct[:], T.prm[:, 0, :, :], 1.0 / 2048, 0.5625, ALU.mult, ALU.add, 256, pr, ["pct"])
-    vt(T.pc[:], T.pct[:], T.prm[:, 1, :, :], ALU.add, 256, ["pct"] + pr, ["pc"])
-    vc(T.pdh[:], T.prm[:, 0, :, :], 256, pr, ["pdh"])
-    vs(T.zp[:], T.uu[:], cf[:, 6:7], cf[:, 14:15], ALU.is_equal, ALU.mult, 144, ["uu", "c6", "wp"], ["zp"])
-    vs(T.zm[:], T.uu[:], cf[:, 6:7], cf[:, 13:14], ALU.is_equal, ALU.mult, 144, ["uu", "c6", "wm"], ["zm"])
-    vs(T.zc[:], T.uu[:], cf[:, 6:7], 2.0 ** 21, ALU.is_equal, ALU.mult, 144, ["uu", "c6"], ["zc"])
-    vm(T.rst[:], 0.0, 256, ["rst"])
-    vm(T.rst[:, 0::4], 1e20, 64, ["rst"])
-    vs(T.bs[:], T.bs0[:], cf[:, 0:1], None, ALU.add, None, 64, ["bs0", "cf"], ["bs"])
-    vs(T.ob8[:], T.ob[:], 0.125, None, ALU.mult, None, 4, ["ob"], ["ob8"])
-    vs(T.nth[:, 0:1], T.tht[:, 0:1], -1.0, None, ALU.mult, None, 1, ["th"], ["nth"])
+    vc("pdh", T.pdh[:], T.prm[:, 0, :, :], pr)
+    vs("pct", T.pct[:], T.prm[:, 0, :, :], 1.0 / 2048, 0.5625, ALU.mult, ALU.add, pr)
+    vt("pc", T.pc[:], T.pct[:], T.prm[:, 1, :, :], ALU.add, ["pct"] + pr)
+    vs("pq0", T.pdq[:, 0, :, :], T.prm[:, 0, :, :], 2032, None, ALU.bitwise_and, None, pr)
+    vs("pq1", T.pdq[:, 1, :, :], T.pdq[:, 0, :, :], 1024.0, None, ALU.min, None, ["pq0"])
+    vt("pq2", T.pdq[:, 2, :, :], T.pdq[:, 1, :, :], T.prm[:, 0, :, :], ALU.add, ["pq1"] + pr)
+    vc("pdm", T.pdm[:], T.pdq[:, 2, :, :], ["pq2"])
+    vs("sm0", T.snq[:, 1, :], T.snr[:, 1, :], 2032, None, ALU.bitwise_and, None, sr)
+    vt("sm1", T.snq[:, 2, :], T.snq[:, 1, :], T.snr[:, 1, :], ALU.add, ["sm0"] + sr)
+    vs("snm", T.snm[:], T.snq[:, 2, :], 16.0, None, ALU.add, None, ["sm1"])
+    vs("zp", T.zp[:], T.uu[:], cf[:, 6:7], cf[:, 14:15], ALU.is_equal, ALU.mult, ["uu", "c6", "wp"])
+    vs("zm", T.zm[:], T.uu[:], cf[:, 6:7], cf[:, 13:14], ALU.is_equal, ALU.mult, ["uu", "c6", "wm"])
+    vs("zc", T.zc[:], T.uu[:], cf[:, 6:7], 2.0 ** 22, ALU.is_equal, ALU.mult, ["uu", "c6"])
+    vm("cen", T.cen[:], -64.0 * 256)
+    vm("rst", T.rst[:], 0.0)
+    vm("rs4", T.rst[:, 0::4], 1e20, ["rst"])
+    act("ob8", T.ob8[:], T.ob[:], ACT.Identity, 0.0, 0.125, ["ob"])
+    act("nth", T.tht[:, 1:2], T.tht[:, 0:1], ACT.Identity, 0.0, -1.0, ["th"])
 
     def extract(z, src, out, q, stop):
-        c0, c1, _ = chunks[q]
-        return [(out[:, c0:c1], z[:, 15 - i:143 - i], src[:, 16 * c0 + i:16 * c1:16], False, stop and i == 15) for i in range(16)]
+        c0, c1 = chunks[q]
+        return [(out, z[:, 15 - i:143 - i], src[:, 16 * c0 + i:16 * c1:16], False, stop and i == 15) for i in range(16)]
+
+    def keycols(c0, c1):
+        return (T.key[:, c0:c1], "key") if c0 < CUT else (T.pay[:, 3, 256 + c0 - CUT:256 + c1 - CUT], "pay3")
+
+    def start_key(c0, c1, s, t):
+        key, bank = keycols(c0, c1)
+        mm("kc" + s, [(key, T.id14[:], T.kc[:, c0:c1], True, False)] + ([(key, T.id14[:], T.cen[:, c0:c1], False, False)] if t == 0 else []),
+           ["id14", "kcol", "cen"], within("key", c0, c1), [bank])
 
     for t in range(NT):
+        now[0] = t
         hw, mw = T["hw%d" % t], T["mw%d" % t]
         last = t == NT - 1
-        for p, (c0, c1, qs) in enumerate(parts):
-            mm([(T["key%d" % p][:, c0:c1], T.ident[:], T.kc[:, c0:c1], True, False)], 4 * (c1 - c0), ["ident", "kc"],
-               ["kc%d" % p] + ["key%d" % q for q in qs], ["key%d" % p])
-        for q, (c0, c1, p) in enumerate(chunks):
-            n, k, bank, cs = 16 * (c1 - c0), str(q), "pay%d" % P["bank"][q], slice(c0, c1)
-            pay, wd = T[bank][:, cs], c1 - c0
-            copy("SV", T.g2[:, 16 * c0:16 * c1], mw[:].indirect(T.pdm[:, cs]), n, mk(t) + ["mwr%d" % t, "pdm"], ["g2" + k], f=gat)
-            mm([(pay, T.ident[:], T.pc[:, cs], True, False)], 4 * max(wd, 64), ["ident", "pc"], ["payc" + k, "pay" + k, "grp" + bank], [bank])
-            mm(extract(T.zp, T.g2, T[bank], q, True), 16 * max(wd, 64), ["zp", "g2" + k], ["pay" + k, "grp" + bank], [bank])
+        start_key(0, CUT, "", t)
+        for q, (c0, c1) in enumerate(chunks):
+            k, bank, cs, js = str(q), "pay%d" % (c0 // 64), slice(c0, c1), slice(16 * c0, 16 * c1)
+            pay = T.pay[:, c0 // 64, c0 % 64:c0 % 64 + c1 - c0]
+            if t == 0: copy("dig" + k, T.g2[:, js], mw[:, 0:1792].indirect(T.pdh[:, cs]), ["own", "mr0", "pdh"])
+            else: copy("dig" + k, T.g2[:, js], mw[:].indirect(T.pdm[:, cs]), ["tr%d" % t, "tr%db" % t, "mr%d" % t, "pdm"])
+            mm("pc" + k, [(pay, T.ident[:], T.pc[:, cs], True, False)], ["ident", "pc"], ["pay" + k, "grp" + bank], [bank])
+            mm("xa" + k, extract(T.zp, T.g2, pay, q, True), ["zp", "dig" + k], ["pay" + k, "grp" + bank], [bank])
             if t == 0:
-                vs(T.ai[:, 0, cs], pay, MAGIC, MAGIC + 1, ALU.add, ALU.subtract, wd, ["pay" + k], ["ai0" + k], [bank])
-                vs(T.ai[:, 1, cs], T.ai[:, 0, cs], NA - 1, None, ALU.bitwise_and, None, wd, ["ai0" + k], ["ai1" + k])
-                vc(T.al[:, cs], T.ai[:, 1, cs], wd, ["ai1" + k], ["al" + k])
+                vs("ai" + k, T.ai[:, 0, cs], pay, MAGIC, MAGIC + 1, ALU.add, ALU.subtract, ["pay" + k], None, [bank])
+                vs("am" + k, T.ai[:, 1, cs], T.ai[:, 0, cs], NA - 1, None, ALU.bitwise_and, None, ["ai" + k])
+                vc("al" + k, T.al[:, cs], T.ai[:, 1, cs], ["am" + k])
             else:
-                vs(T.al[:, cs], pay, MAGIC, MAGIC + 1, ALU.add, ALU.subtract, wd, ["pay" + k], ["al" + k], [bank])
-            mm(extract(T.zm, T.g2, T["key%d" % p], q, False), 16 * max(wd, 64), ["zm", "g2" + k], ["keym" + k, "key" + k], ["key%d" % p])
+                vs("al" + k, T.al[:, cs], pay, MAGIC, MAGIC + 1, ALU.add, ALU.subtract, ["pay" + k], None, [bank])
             win = T.wav[:, 0:NA] if t == 0 else T.wav[:]
-            copy("SV", T.wb[:, 16 * c0:16 * c1], win.indirect(T.al[:, cs]), n, ["wv0", "al" + k] + ([] if t == 0 else ["wv1"]), ["wb" + k], f=gat)
+            copy("wg" + k, T.wb[:, js], win.indirect(T.al[:, cs]), ["wv0", "al" + k] + ([] if t == 0 else ["wv1"]))
+        start_key(CUT, 256, "b", t)
+        for q, (c0, c1) in enumerate(chunks):
+            mm("xm%d" % q, extract(T.zm, T.g2, keycols(c0, c1)[0], q, False), ["zm", "dig%d" % q], ["key%d" % q], [keycols(c0, c1)[1]])
         if t == 0:
-            dma("Y", T.wav[:, NA:2 * NA], T.wv[:], 1048576, ["hr0"], ["wv1"])
-        for q, (c0, c1, p) in enumerate(chunks):
-            n, k, js = 16 * (c1 - c0), str(q), slice(16 * c0, 16 * c1)
-            vt(T.prod[:, js], hw[:].indirect(T.pdh[:, c0:c1]), T.wb[:, js], ALU.mult, n, hk(t) + ["hr%d" % t, "pdh", "wb" + k], ["prod" + k], f=gat)
-            act(T.ab[:, js], T.prod[:, js], ACT.Abs, T.ob[:, t:t + 1], -1.0, n, ["prod" + k, "ob"], ["ab" + k])
-            mode = P["p2"][q]
-            if mode == "V":
-                vs(T.cmp[:, js], T.ab[:, js], T.tht[:, 0:1], None, ALU.is_gt, None, n, ["ab" + k, "th"], ["cmp" + k])
+            dma("wv1", "Y", T.wav[:, NA:2 * NA], T.wv[:], ["hr0"])
+        for q, (c0, c1) in enumerate(chunks):
+            k, js = str(q), slice(16 * c0, 16 * c1)
+            if q in H_ON_SCALAR:
+                n = 16 * (c1 - c0)
+                copy("hq" + k, T.hq[:, 0:n], hw[:].indirect(T.pdh[:, c0:c1]), hk(t) + ["hr%d" % t, "pdh"], ["hq"])
+                mm("wq" + k, [(T.hs[:, b, :], T.idb[:], T.wb[:, 16 * c0 + 512 * b:16 * c0 + 512 * b + 512], True, True) for b in range(n // 512)],
+                   ["idb", "wg" + k], ["hs0", "hs1"], ["hs0", "hs1"])
+                vt("pr" + k, T.prod[:, js], T.hs[:, 0:n // 512, :], T.hq[:, 0:n], ALU.mult, ["hq", "hs0", "hs1"], None, ["hs0", "hs1"])
             else:
-                act(T.sg[:, js], T.ab[:, js], ACT.Sign, T.nth[:, 0:1], 1.0, n, ["ab" + k, "nth"], ["sg" + k])
-                if mode == "S":
-                    vs(T.cmp[:, js], T.sg[:, js], 0.0, None, ALU.max, None, n, ["sg" + k], ["cmp" + k], f=0.5)
-                else:
-                    act(T.cmp[:, js], T.sg[:, js], ACT.Relu, 0.0, 1.0, n, ["sg" + k], ["cmp" + k])
-            c0, c1, qs = parts[p]
-            kk = ["key%d" % j for j in qs]
-            mm(extract(T.zc, T.cmp, T["key%d" % p], q, q == qs[-1]), 16 * max(n // 16, 64), ["zc", "cmp" + k] + (kk if q == qs[-1] else []),
-               ["key" + k], ["key%d" % p])
-            if q != qs[-1]: continue
-            wd, nb, b0 = c1 - c0, (c1 - c0) // 4, c0 // 4
-            bs, cs, s = slice(b0, b0 + nb), slice(c0, c1), str(p)
-            key = T["key" + s][:, cs]
-            op("V", lambda e, cs=cs, key=key: g.vector.tensor_tensor_scan(T.rr[:, cs], T.rst[:, cs], key, 0.0, ALU.add, ALU.min),
-               kk + ["rst"], ["rr" + s], ["key" + s], cv(wd))
-            vt(T.dd[:, cs], key, T.rr[:, cs], ALU.subtract, wd, kk + ["rr" + s], ["dd" + s], ["key" + s], f=1.0)
-            vs(T.xx[:, bs, 0], T.rr[:, c0 + 3:c1:4], 2.0 ** -10, None, ALU.mult, None, nb, ["rr" + s], ["x0" + s])
-            runs = []
-            for j in qs:
-                if runs and P["bank"][runs[-1][0]] == P["bank"][j]: runs[-1].append(j)
-                else: runs.append([j])
-            for r in runs:
-                a0, a1, bank = chunks[r[0]][0], chunks[r[-1]][1], "pay%d" % P["bank"][r[0]]
-                vt(T.d1[:, a0:a1], T[bank][:, a0:a1], T.dd[:, a0:a1], ALU.subtract, a1 - a0, ["pay%d" % j for j in r] + ["dd" + s],
-                   ["d1%d" % j for j in r], [bank], f=1.0)
-            vs(T.lq[:, 0, bs], T.xx[:, bs, 0], 48, None, ALU.bitwise_and, None, nb, ["x0" + s], ["lq0" + s])
-            op("V", lambda e, cs=cs: g.vector.tensor_tensor_scan(T.ss[:, cs], T.dd[:, cs], T.d1[:, cs], 0.0, ALU.min, ALU.max),
-               ["dd" + s] + ["d1%d" % j for j in qs], ["ss" + s], (), cv(wd))
-            vt(T.lq[:, 1, bs], T.lq[:, 0, bs], T.bs[:, 0:nb], ALU.add, nb, ["lq0" + s, "bs"], ["lq1" + s])
-            vs(T.xx[:, bs, 1], T.ss[:, c0 + 3:c1:4], 2048.0, -1152.0, ALU.mult, ALU.add, nb, ["ss" + s], ["x1" + s])
-            if not last:
-                vs(T.dg[:, bs, 1], T.xx[:, bs, 0], 19, None, ALU.arith_shift_right, None, nb, ["x0" + s], ["dg1" + s])
-                vs(T.dg[:, bs, 0::2], T.xx[:, bs, :], 11, 255, ALU.arith_shift_right, ALU.bitwise_and, 2 * nb, ["x0" + s, "x1" + s], ["dg0" + s, "dg2" + s])
-                vs(T.dg[:, bs, 3], T.xx[:, bs, 1], 19, 3, ALU.arith_shift_right, ALU.bitwise_and, nb, ["x1" + s], ["dg3" + s])
-            vs(T.lq[:, 2, bs], T.xx[:, bs, 1], 2047, None, ALU.bitwise_and, None, nb, ["x1" + s], ["lq2" + s])
-            vc(T.lu[:, 2 * b0:2 * b0 + 2 * nb], T.lq[:, 1:3, bs], 2 * nb, ["lq1" + s, "lq2" + s], ["lu" + s])
-            if not last:
-                spread([p], t + 1)
-                if p == NP - 1: first = show_m(t + 1)
-            ws = slice(16 * c0, 16 * c1)
-            for u, (u0, u1, pu) in enumerate(pieces):
-                if pu != p: continue
-                pick, pds = T.lu[:, b0 + u0:b0 + u1], T.lu[:, b0 + nb + u0:b0 + nb + u1]
-                vsl, m, su = slice(16 * u0, 16 * u1), 16 * (u1 - u0), str(u)
-                act(T.ep[:, vsl], T.prod[:, ws].indirect(pick), ACT.Identity, T.ob8[:, t:t + 1], -0.125, m,
-                    ["prod%d" % j for j in qs] + ["lu" + s, "ob8"], ["ep" + su], f=gat)
-                vt(T.tb[:, vsl], T.wb[:, ws].indirect(pick), T.ep[:, vsl], ALU.mult, m, ["wb%d" % j for j in qs] + ["lu" + s, "ep" + su],
-                   ["tb" + su], f=gat)
-                dst = T.hout if last else T["hw%d" % (t + 1)]
-                vt(dst[:, vsl], hw[:].indirect(pds), T.tb[:, vsl], ALU.add, m, hk(t) + ["hr%d" % t, "lu" + s, "tb" + su], [hk(t + 1)[u]], f=gat)
-                if last:
-                    dma("Y", T.yh[:, vsl], T.hout[:, vsl], 512 * m, [hk(t + 1)[u]], ["yh" + su])
+                vt("pr" + k, T.prod[:, js], hw[:].indirect(T.pdh[:, c0:c1]), T.wb[:, js], ALU.mult, hk(t) + ["hr%d" % t, "pdh", "wg" + k])
+            act("ab" + k, T.ab[:, js], T.prod[:, js], ACT.Abs, T.ob[:, t:t + 1], -1.0, ["pr" + k, "ob"])
+            if q in ON_SCALAR[last]:
+                act("sg" + k, T.sg[:, js], T.ab[:, js], ACT.Sign, T.tht[:, 1:2], 1.0, ["ab" + k, "nth"])
+                act("cm" + k, T.cmp[:, js], T.sg[:, js], ACT.Relu, 0.0, 1.0, ["sg" + k])
+            else:
+                vs("cm" + k, T.cmp[:, js], T.ab[:, js], T.tht[:, 0:1], None, ALU.is_gt, None, ["ab" + k, "th"])
+            (key, bank), end = keycols(c0, c1), k == CLOSE or c1 == 256
+            mm("xc" + k, extract(T.zc, T.cmp, key, q, end), ["zc", "cm" + k], ["key" + k], [bank])
+        for a, b in ((0, CUT), (CUT, 256)):
+            group = [j for j, o in enumerate(ops) if o["name"] in [(t, nm) for nm in within("xc", a, b) + within("xm", a, b)]]
+            close = [j for j in group if ops[j]["name"][1] == ("xc" + CLOSE if a == 0 else within("xc", a, b)[-1])][0]
+            ops[close]["deps"].update(j for j in group if j != close)
+            for nm in within("key", a, b): lastw[nm] = close
+        split = SPLIT_LAST if last else SPLIT
+        def scan(name, out, d0, d1, o0, o1, r, w, banks):
+            op(name, "V", lambda e: g.vector.tensor_tensor_scan(out, d0, d1, 0.0, o0, o1), r, w, banks)
+        for c0, c1, s, k in spans("rr", split):
+            key, bank = keycols(c0, c1)
+            scan("rr" + s, T.rr[:, c0:c1], T.rst[:, c0:c1], key, ALU.add, ALU.min, within("key", c0, c1) + ["rst"], k("rr"), [bank])
+            vt("dd" + s, T.dd[:, c0:c1], key, T.rr[:, c0:c1], ALU.subtract, within("key", c0, c1) + k("rr"), k("dd"), [bank])
+        for c0, c1, s, k in spans("d1", split):
+            vt("d1" + s, T.d1[:, c0:c1], T.pay[:, c0 // 64:c1 // 64, 0:64], T.dd[:, c0:c1], ALU.subtract, within("pay", c0, c1) + k("dd"), k("d1"),
+               ["pay%d" % b for b in range(c0 // 64, c1 // 64)])
+            scan("ss" + s, T.ss[:, c0:c1], T.dd[:, c0:c1], T.d1[:, c0:c1], ALU.min, ALU.max, k("dd", "d1"), k("ss"), ())
+        for c0, c1, s, k in spans("pk", split):
+            bs = slice(c0 // 4, c1 // 4)
+            vs("x0" + s, T.xx[:, bs, 0], T.rr[:, c0 + 3:c1:4], 2.0 ** -11, None, ALU.mult, None, k("rr"), k("x0"))
+            vs("pk1" + s, T.lq[:, 0, bs], T.xx[:, bs, 0], 2040, None, ALU.bitwise_and, None, k("x0"), k("pk1"))
+            vs("pk" + s, T.lu[:, bs], T.lq[:, 0, bs], 2.0, cf[:, 3:4] if c0 else cf[:, 0:1], ALU.mult, ALU.add, k("pk1") + ["cf", "cpb"], k("pk"))
+        for c0, c1, s, k in spans("pd", split):
+            bs = slice(c0 // 4, c1 // 4)
+            vs("x1" + s, T.xx[:, bs, 1], T.ss[:, c0 + 3:c1:4], 2048.0, -1152.0, ALU.mult, ALU.add, k("ss"), k("x1"))
+            vs("pd1" + s, T.lq[:, 1, bs], T.xx[:, bs, 1], 2047, None, ALU.bitwise_and, None, k("x1"), k("pd1"))
+            vc("pdl" + s, T.lu[:, 64 + c0 // 4:64 + c1 // 4], T.lq[:, 1, bs], k("pd1"), k("pdl"))
         if not last:
-            show_h(t + 1, first)
+            for c0, c1, s, k in spans("dg", split):
+                bs = slice(c0 // 4, c1 // 4)
+                vs("dlo" + s, T.dg[:, bs, 0::2], T.xx[:, bs, :], 11, 255, ALU.arith_shift_right, ALU.bitwise_and, k("x0", "x1"), k("dg0", "dg2"))
+                vs("dMh" + s, T.dg[:, bs, 1], T.xx[:, bs, 0], 19, None, ALU.arith_shift_right, None, k("x0"), k("dg1"))
+                vs("dmh" + s, T.dg[:, bs, 3], T.xx[:, bs, 1], 19, 3, ALU.arith_shift_right, ALU.bitwise_and, k("x1"), k("dg3"))
+            show_m(t + 1, split)
+        for u, (u0, u1) in enumerate(cuts(LAST_PIECES if last else PIECES)):
+            c0, c1, s, k = [x for x in spans("pk", split) if x[0] <= 4 * u0 < x[1]][0]
+            kd = [x for x in spans("pd", split) if x[0] <= 4 * u0 < x[1]][0][3]
+            pick, pds = T.lu[:, u0:u1], T.lu[:, 64 + u0:64 + u1]
+            vsl, ws, su = slice(16 * u0, 16 * u1), slice(16 * c0, 16 * c1), str(u)
+            free = hk(t)
+            act("ep" + su, T.ep[:, vsl], T.prod[:, ws].indirect(pick), ACT.Identity, T.ob8[:, t:t + 1], -0.125, within("pr", c0, c1) + k("pk") + ["ob8"] + free)
+            dst = T.hout if last else T["hw%d" % (t + 1)]
+            new, mode = "h%d_%d" % (t + 1, u), VIA_PSUM[last][u]
+            ps, bank = T.pay[:, u, 0:16 * (u1 - u0)], ["pay" + su]
+            if mode == 0:
+                vt("tb" + su, T.tb[:, vsl], T.wb[:, ws].indirect(pick), T.ep[:, vsl], ALU.mult, within("wg", c0, c1) + k("pk") + ["ep" + su] + free)
+            else:
+                copy("ws" + su, T.wsl[:, vsl], T.wb[:, ws].indirect(pick), within("wg", c0, c1) + k("pk") + free)
+                mm("wp" + su, [(ps, T.idb[:], T.wsl[:, vsl], True, True)], ["idb", "ws" + su], ["pay" + su], bank)
+                vt("tb" + su, ps if mode == 2 else T.tb[:, vsl], ps, T.ep[:, vsl], ALU.mult, ["pay" + su, "ep" + su] + free,
+                   ["tb" + su, "pay" + su] if mode == 2 else None, bank)
+            if mode < 2:
+                vt("hn" + su, dst[:, vsl], hw[:].indirect(pds), T.tb[:, vsl], ALU.add, hk(t) + ["hr%d" % t, "tb" + su] + kd("pdl"), [new])
+            else:
+                copy("hp" + su, T.tb[:, vsl], hw[:].indirect(pds), hk(t) + ["hr%d" % t] + kd("pdl") + free)
+                vt("hn" + su, dst[:, vsl], ps, T.tb[:, vsl], ALU.add, ["hp" + su, "tb" + su, "pay" + su], [new], bank)
+            if last:
+                dma("yh" + su, "Y", T.yh[:, vsl], T.hout[:, vsl], [new])
+            else:
+                move(u, dst, vsl, new)
+        if not last:
+            show_h(t + 1, ["hm%d" % u + x for u in range(len(PIECES)) for x in ("", "x")])
 
-    xr = allp("x0") + allp("x1")
-    vs(T.xp[:, 0, :], T.xx[:, :, 0], 11, None, ALU.arith_shift_right, None, 64, xr, ["xp0", "xp1"])
-    vs(T.xp[:, 1, :], T.xx[:, :, 1], 11, NA - 1, ALU.arith_shift_right, ALU.bitwise_and, 64, xr, ["xp2", "xp3"])
-    vc(T.ff[:], T.xp[:], 128, ["xp0", "xp2"], ["ff"])
+    vs("xM", T.xp[:, 0, :], T.xx[:, :, 0], 11, None, ALU.arith_shift_right, None, ["x0", "x0b"])
+    vs("xm", T.xp[:, 1, :], T.xx[:, :, 1], 11, NA - 1, ALU.arith_shift_right, ALU.bitwise_and, ["x1", "x1b"])
+    vs("fM", T.ff[:, 0, :], T.xp[:, 0, :], 64.0, None, ALU.add, None, ["xM"])
+    vc("fm", T.ff[:, 1, :], T.xp[:, 1, :], ["xm"])
     for b in range(4):
         for x, col in enumerate((cf[:, 12:13], cf[:, 1:2])):
             def fn(e, b=b, x=x, col=col):
                 if e == "V": return g.vector.tensor_scalar(T.t2i[:, b::4, x, :], T.ff[:, :, b::4], col, None, ALU.mult)
                 return g.scalar.activation(T.t2i[:, b::4, x, :], T.ff[:, :, b::4], ACT.Identity, scale=col)
-            op("SV", fn, ["ff", "c12", "cf", "t2o"], ["tj%d%d" % (b, x)], (), cv(32))
-    op("V", lambda e: g.vector.transpose(T.t2o[:], T.t2i[:]), ["tj%d%d" % (b, x) for b in range(4) for x in range(2)], ["t2o"], (), cv(256))
-    vt(T.no[:], T.t2o[:, :, 0, :], T.t2o[:, :, 1, :], ALU.add, 128, ["t2o"], ["no"])
-    dma("Y", T.ymt[:], T.no[:, 0:4, :], 32768, ["no"], ["ymt"])
-    dma("S", T.ymm[:], T.no[:, 4:8, :], 32768, ["no"], ["ymm"])
+            op("tj%d" % (2 * b + x), "VS", fn, ["fM", "fm", "c12", "cf"], ["tj%d" % (2 * b + x)])
+    op("t2", "V", lambda e: g.vector.transpose(T.t2o[:], T.t2i[:]), ["tj%d" % j for j in range(8)], ["t2"])
+    vt("no", T.no[:], T.t2o[:, :, 0, :], T.t2o[:, :, 1, :], ALU.add, ["t2"])
+    dma("ymt", "Y", T.ymt[:], T.no[:, 0:4, :], ["no"])
+    dma("ymm", "S", T.ymm[:], T.no[:, 4:8, :], ["no"])
     return ops
 
 
-def schedule(ops, P):
-    n, lat = len(ops), P["lat"]
-    if P["order"]:
-        for i, k in enumerate(P["order"]):
-            ops[k]["eng"] = P["eng"][k].strip(); ops[k]["start"] = ops[k]["fin"] = float(i)
-        return list(P["order"])
-    succ = [[] for _ in ops]
+def queues(ops, order):
+    at = {o["name"]: k for k, o in enumerate(ops)}
+    qs = {e: [] for e in "VSPGY"}
     for k, o in enumerate(ops):
-        for d in o["deps"]: succ[d].append(k)
-    rnd = [P["seed"]]
-    def rand():
-        rnd[0] = (rnd[0] * 6364136223846793005 + 1442695040888963407) % (1 << 64)
-        return (rnd[0] >> 33) / float(1 << 31)
-
-    lev = [0.0] * n
-    for k in range(n - 1, -1, -1):
-        lev[k] = ops[k]["cost"] + ops[k]["done"] + lat + max([lev[j] for j in succ[k]] + [0.0])
-
-    def run(w, pick):
-        busy = {e: [] for e in "VSPGY"}
-        fin, start, eng = [0.0] * n, [0.0] * n, [""] * n
-        pri = [lev[k] + w.get(o["tag"], 0.0) for k, o in enumerate(ops)]
-        missing = [len(o["deps"]) for o in ops]
-        cand = [k for k in range(n) if not missing[k]]
-        while cand:
-            k = max(cand, key=lambda j: pri[j]); cand.remove(k)
-            for j in succ[k]:
-                missing[j] -= 1
-                if not missing[j]: cand.append(j)
-            o = ops[k]; c = o["cost"]
-            ready = max([fin[d] + lat for d in o["deps"]] + [0.0])
-            best = (ready, "", 0)
-            for e in (pick.get(o["tag"]) or o["engs"]):
-                st, bz = ready, busy[e]
-                i = len(bz)
-                while i > 0 and bz[i - 1][1] > ready: i -= 1
-                while i < len(bz) and bz[i][0] < st + c:
-                    st = max(st, bz[i][1]); i += 1
-                if best[1] == "" or st < best[0]: best = (st, e, i)
-            st, e, i = best
-            if e: busy[e].insert(i, (st, st + c))
-            start[k], eng[k], fin[k] = st, e, st + c + o["done"]
-        return max(fin), start, eng, fin
-
-    free = sorted(set(o["tag"] for o in ops if len(o["engs"]) > 1))
-    tags = sorted(set(o["tag"] for o in ops))
-    big = sorted(set(o["tag"] for o in ops if o["cost"] > 400))
-    w, pick = dict(P["w"]), dict(P["pick"])
-    cur = best = run(w, pick)
-    keep = (w, pick)
-    for it in range(P["iters"]):
-        w2, p2 = dict(w), dict(pick)
-        for _j in range(1 + int(3 * rand())):
-            x = rand()
-            if free and x < 0.25:
-                p2[free[int(rand() * len(free))]] = "VS"[int(2 * rand())]
-            else:
-                pool = big if x < 0.75 else tags
-                w2[pool[int(rand() * len(pool))]] = float(int(16000 * (rand() - 0.5) * (0.2 + rand())))
-        r = run(w2, p2)
-        if r[0] <= cur[0] + 600.0 * (1 - it / P["iters"]) * rand():
-            cur, w, pick = r, w2, p2
-            if r[0] < best[0]: best, keep = r, (w2, p2)
-    P["found"] = keep
-    for k, o in enumerate(ops):
-        o["start"], o["eng"], o["fin"] = best[1][k], best[2][k], best[3][k]
-    return sorted(range(n), key=lambda k: (best[1][k], k))
+        if o["kind"] == "d" and o["engs"] == "S" and o["name"][0] < 0: qs["S"].append(k)
+        if o["engs"] in ("G", "Y"): qs[o["engs"]].append(k)
+    for e, (start, step, last) in order.items():
+        for t in range(-1, NT):
+            for nm in (start if t < 0 else step if t < NT - 1 else last).split():
+                k = at.get((t - nm.endswith("-"), nm.rstrip("-")))
+                if k is not None and not (t == 0 and nm.endswith("-")): qs[e].append(k)
+    qs["S"].append(at[(NT - 1, "ymm")])
+    return qs
 
 
-def emit(g, T, ops, seq):
+def emit(g, T, ops, qs):
     queue = {"V": g.vector, "S": g.scalar, "P": g.tensor, "G": g, "Y": g.sync}
     qsem = {"V": "qv", "S": "qs", "P": "qp", "G": "qg"}
+    seq, done, head = [], set(), {e: 0 for e in qs}
+    arrivals = [k for k, o in enumerate(ops) if o["kind"] == "a"]
+    while len(seq) < len(ops):
+        ready = [(k, "") for k in arrivals if k not in done] + [(qs[e][head[e]], e) for e in qs if head[e] < len(qs[e])]
+        k, e = [(k, e) for k, e in ready if ops[k]["deps"] <= done][0]
+        seq.append(k); done.add(k); ops[k]["eng"] = e
+        if e: head[e] += 1
+    place = {k: i for i, k in enumerate(seq)}
     pos, cnt, ndma = {}, {e: 0 for e in queue}, 0
     known = {e: {} for e in queue}
     snap, waits, need = {}, {}, set()
@@ -437,7 +454,7 @@ def emit(g, T, ops, seq):
         if o["kind"] == "a":
             pos[k] = (o["fn"][0], 1); snap[k] = {o["fn"][0]: 1}; continue
         e = o["eng"]; kn = known[e]; w = []
-        for d in sorted(o["deps"], key=lambda d: -ops[d]["fin"]):
+        for d in sorted(o["deps"], key=lambda d: -place[d]):
             od = ops[d]
             if od["kind"] == "r" or (e == "P" and od["eng"] == "P"): continue
             s, v = pos[d]
@@ -474,6 +491,9 @@ def emit(g, T, ops, seq):
 
 def rank_program(g, core, T, topo):
     if T.rank_of(core) is None:
+        for rank in range(NR):
+            for d in HANDED:
+                if helper(T, topo, rank, d) == core: hand_on(g, core, T, topo, rank, d)
         return
-    ops = plan(g, core, T, topo, PARAM)
-    emit(g, T, ops, schedule(ops, PARAM))
+    ops = plan(g, core, T, topo)
+    emit(g, T, ops, queues(ops, ORDER))

from concourse.bass import DstId, RemoteDMATransfer
from concourse.mybir import AluOpType, ActivationFunctionType

ALU = AluOpType
ACT = ActivationFunctionType
NR, NV, NS, NA, NT = 4, 1024, 256, 4096, 4
MAGIC = 12582912.0

F, B, I, U = "float32", "bfloat16", "int32", "uint16"
SCRATCH = {
    "wav": ("sbuf", [128, 2 * NA], B),
    "g2": ("sbuf", [128, 4096], B), "wb": ("sbuf", [128, 4096], B), "prod": ("sbuf", [128, 4096], F),
    "ab": ("sbuf", [128, 4096], F), "cmp": ("sbuf", [128, 4096], B), "sg": ("sbuf", [128, 4096], B),
    "ep": ("sbuf", [128, 1024], F), "tb": ("sbuf", [128, 1024], F), "hout": ("sbuf", [128, 1024], F),
    "hmv": ("sbuf", [128, 1024], F), "wsl": ("sbuf", [128, 1024], B), "hq": ("sbuf", [128, 1024], F),
    "tin": ("sbuf", [128, 64, 32], B), "mwq": ("sbuf", [128, 2048], B),
    "raw": ("sbuf", [128, 2, 4, 64], I), "prm": ("sbuf", [128, 2, 64, 4], I),
    "snr": ("sbuf", [128, 2, 48], I), "snq": ("sbuf", [128, 3, 48], I), "snf": ("sbuf", [128, 2, 48], F),
    "snh": ("sbuf", [128, 48], U), "snm": ("sbuf", [128, 48], U), "sn0": ("sbuf", [128, 48], U),
    "pdq": ("sbuf", [128, 3, 64, 4], I), "pdh": ("sbuf", [128, 256], U), "pdm": ("sbuf", [128, 256], U),
    "pct": ("sbuf", [128, 64, 4], F), "pc": ("sbuf", [128, 256], F),
    "al": ("sbuf", [128, 256], U), "ai": ("sbuf", [128, 2, 256], I),
    "ob": ("sbuf", [128, 4], F), "ob8": ("sbuf", [128, 4], F), "tht": ("sbuf", [128, 4], F),
    "mmi": ("sbuf", [128, 2, 64], I), "t2i": ("sbuf", [128, 8, 2, 16], F), "t2o": ("sbuf", [128, 8, 2, 16], F),
    "xp": ("sbuf", [128, 2, 64], I), "ff": ("sbuf", [128, 2, 64], F), "no": ("sbuf", [128, 8, 16], F),
    "pi": ("sbuf", [128, 4], I), "ci": ("sbuf", [128, 4], I), "cf": ("sbuf", [128, 16], F),
    "uu": ("sbuf", [128, 144], F), "zc": ("sbuf", [128, 144], B), "zm": ("sbuf", [128, 144], B), "zp": ("sbuf", [128, 144], B),
    "zero": ("sbuf", [128, 128], B), "idb": ("sbuf", [128, 128], B), "ident": ("sbuf", [128, 128], F), "id14": ("sbuf", [128, 128], B),
    "sh1": ("sbuf", [128, 128], B), "shb": ("sbuf", [128, 128], B), "shf": ("sbuf", [128, 128], F),
    "kc": ("sbuf", [128, 256], B), "cen": ("sbuf", [128, 256], B), "rst": ("sbuf", [128, 256], F),
    "nat0": ("sbuf", [128, 64], I), "nat": ("sbuf", [128, 64], U),
    "rr": ("sbuf", [128, 256], F), "dd": ("sbuf", [128, 256], F), "d1": ("sbuf", [128, 256], F), "ss": ("sbuf", [128, 256], F),
    "xx": ("sbuf", [128, 64, 2], I), "dg": ("sbuf", [128, 64, 4], I),
    "lq": ("sbuf", [128, 2, 64], I), "lu": ("sbuf", [128, 128], U),
    "pay": ("psum", [128, 4, 512], F), "key": ("psum", [128, 512], F),
    "hs": ("psum", [128, 2, 512], F), "hs2": ("psum", [128, 512], F),
}
for _t in range(NT):
    SCRATCH["hw%d" % _t] = ("sbuf", [128, 1792], F)
    SCRATCH["mw%d" % _t] = ("sbuf", [128, 2816], B)
    SCRATCH["hsn%d" % _t] = ("sbuf", [128, 768], F)
    SCRATCH["msn%d" % _t] = ("sbuf", [128, 768], B)

NDMA = 40
SEMAPHORES = ["qv", "qs", "qp", "qg", "sent"] + ["dm%d" % k for k in range(NDMA)] + \
             ["am%d" % t for t in range(NT)] + ["ah%d" % t for t in range(NT)] + ["fw%d" % t for t in range(NT)]

CHUNKS = [64, 64, 64, 32, 32]
ON_SCALAR = [[3], [3]]
PIECES = [24, 24, 16]
LAST_PIECES = [24, 24, 16]
MOVE_BY_DMA = []
H_ON_SCALAR = []
VIA_PSUM = [[1, 1, 0], [2, 2, 0]]
CUT, CLOSE = 192, "2"
SPLIT = ["rr", "d1", "pk"]
SPLIT_LAST = ["rr", "d1", "pk", "pd"]
CALLS_M = [[0, 1], [2]]
CALLS_H = [[0, 2], [1]]
HANDED = []

ORDER = {
    "V": ["zero tin0 ci1 ci0 cf dMh dMl dmh dml sq tinA snh su cpb sv w1 sn0 tr w0 ms0 c32 w3 prm0 rst c6 prm2 prm1 nat w2 wm rs4 "
          "prm3 zm pq0 pdh pq1 sm0 c12 sm1 pct pq2 wp snm zp cen zc pc pdm",
          "dig0 dig2 ai0 ai3 ai1 am0 am1 am3 al0 ai2 al3 al1 wg3 ai4 am2 am4 al2 al4 pr3 pr0 pr1 pr2 cm0 pr4 cm1 cm2 cm4 "
          "rr dd x0 d1 pk1 rrb pk ddb x0b d1b pk1b ss ssb pkb x1 dMh dlo dmh pd1 tinA tb0 pdl tb2 tr hn0 tb1 hn1 hn2 hc1 hg0",
          "dig0 al0 dig2 al1 dig4 al2 al3 pr0 pr1 al4 pr2 pr3 pr4 cm0 cm1 cm2 cm4 rr x0 dd pk1 pk d1 rrb ss ddb ws0 x1 d1b pd1 ssb "
          "x0b x1b xM pdl xm pk1b pd1b tb1 fm pdlb pkb tb0 fM hn0 hn1 tb2 hn2 t2 no"],
    "S": ["shf tinB ident id14 ms1 ms2 hc1 hc0 own hg0 hg1 hg2 nth ob8",
          "dig1 dig3 dig4 wg0 wg1 wg2 ab0 ab3 wg4 ab1 ab2 ab4 sg3 cm3 ws0 ep0 ep2 tinB ws1 ep1 ms0 ms1 ms2 hc0 hc2 hg2 hg1",
          "dig3 dig1 wg0 wg1 wg2 wg3 wg4 ab0 ab1 ab4 ab2 ab3 sg3 cm3 ep1 ws1 ep0 hp0 hp1 ep2 tj0 tj1 tj2 tj3 tj4 tj5 tj6 tj7"],
    "P": ["sh hs0 hs1",
          "pc2 pc0 pc1 pc3 kc xa0 xa1 xa3 xa2 pc4 xa4 kcb xm1 xm3 xm4 xm0 xm2 xc0 xc1 xc2 xc3 xc4 wp0 sh wp1 hs0 hs1 hs2",
          "pc0 pc1 pc3 pc2 kc xa0 xa1 xa2 xa3 pc4 xm1 xa4 kcb xm0 xm4 xm3 xm2 xc0 xc1 xc2 xc3 xc4 wp1 wp0"],
}


def helper(T, topo, rank, d):
    core, peer = T.cores[rank], T.cores[(rank + d + 1) % NR]
    able = [c for c in topo.cores_of(core) if topo.die(c) != topo.die(core) and topo.may_write(c, peer)]
    return able[HANDED.index(d) % len(able)]


def on_chip_engines(T, topo, rank, d):
    core, peer = T.cores[rank], T.cores[(rank + d + 1) % NR]
    return [e for e in topo.engines(core, helper(T, topo, rank, d)) if e not in topo.engines(core, peer)]


def hand_on(g, core, T, topo, rank, d):
    peer = T.cores[(rank + d + 1) % NR]
    rid, pid, _ = topo.addr(peer)
    call = [[x for x in ds if x in HANDED] for ds in CALLS_H if d in ds][0]
    for t in range(NT):
        g.wait_ge(T.sem["fw%d" % t], len(on_chip_engines(T, topo, rank, d)) // len(call))
        g.remote_dma(T["hw%d" % t][:, NV + 256 * d:NV + 256 * d + 256], T["hsn%d" % t][:, 256 * d:256 * d + 256], T.sem["ah%d" % t], T.sem.sent,
                     pid, rid, topo.mask(core, peer))
    g.wait_ge(T.sem.sent, NT * len(topo.engines(core, peer)))


def plan(g, core, T, topo):
    rank = T.rank_of(core)
    ops, lastw, readers, bankuse, now = [], {}, {}, {}, [-1]
    ends = [sum(CHUNKS[:q]) for q in range(len(CHUNKS) + 1)]
    chunks = list(zip(ends, ends[1:]))
    def cuts(ws): return [(sum(ws[:u]), sum(ws[:u + 1])) for u in range(len(ws))]
    def hk(t): return ["h%d_%d" % (t, u) for u in range(len(PIECES))] if t else ["h0"]
    def within(name, c0, c1): return [name + str(q) for q, (a, b) in enumerate(chunks) if c0 <= a < c1]
    def spans(name, split):
        def k(sfx): return lambda *names: [nm + x for nm in names for x in sfx]
        return [(0, CUT, "", k([""])), (CUT, 256, "b", k(["b"]))] if name in split else [(0, 256, "", k(["", "b"]))]

    def op(name, engs, fn, reads=(), writes=(), banks=(), kind="c", after=()):
        k = len(ops)
        deps = set(after)
        for r in reads:
            if r in lastw: deps.add(lastw[r])
        for w in writes:
            if w in lastw: deps.add(lastw[w])
            deps.update(readers.get(w, ()))
        for b in banks:
            u = bankuse.setdefault(b, [engs, [], []])
            if u[0] != engs or len(engs) > 1: u[0], u[1], u[2] = engs, [], u[1]
            deps.update(u[2]); u[1].append(k)
        for r in reads: readers.setdefault(r, []).append(k)
        for w in writes:
            lastw[w] = k; readers[w] = []
        deps.discard(k)
        ops.append({"name": (now[0], name), "engs": engs, "fn": fn, "deps": deps, "kind": kind})
        return k

    def vs(name, out, in0, s1, s2, o0, o1, r, w=None, banks=()):
        w = [name] if w is None else w
        if o1 is None: return op(name, "V", lambda e: g.vector.tensor_scalar(out, in0, s1, None, o0), r, w, banks)
        return op(name, "V", lambda e: g.vector.tensor_scalar(out, in0, s1, s2, o0, o1), r, w, banks)
    def vt(name, out, in0, in1, o, r, w=None, banks=()):
        return op(name, "V", lambda e: g.vector.tensor_tensor(out, in0, in1, o), r, [name] if w is None else w, banks)
    def vc(name, out, in_, r, w=None):
        return op(name, "V", lambda e: g.vector.tensor_copy(out, in_), r, [name] if w is None else w)
    def vm(name, out, c, w=None):
        return op(name, "V", lambda e: g.vector.memset(out, c), (), [name] if w is None else w)
    def copy(name, out, in_, r, w=None, banks=()):
        def fn(e):
            return g.vector.tensor_copy(out, in_) if e == "V" else g.scalar.activation(out, in_, ACT.Copy)
        return op(name, "VS", fn, r, [name] if w is None else w, banks)
    def act(name, out, in_, func, bias, scale, r, w=None):
        return op(name, "S", lambda e: g.scalar.activation(out, in_, func, bias=bias, scale=scale), r, [name] if w is None else w)
    def mm(name, lst, r, w, banks):
        def fn(e):
            for a in lst: ins = g.tensor.matmul(*a)
            return ins
        return op(name, "P", fn, r, w, banks)
    def dma(name, q, out, in_, r, w=None):
        def fn(e): return (g.sync if e == "Y" else g.scalar).dma_start(out, in_)
        return op(name, q, fn, r, [name] if w is None else w, (), kind="d")
    def gp(name, fn, r): return op(name, "G", lambda e: fn(), r, [name])

    dma("mt", "Y", T.mmi[:, 0, :], T.mt[:], ())
    dma("mm", "S", T.mmi[:, 1, :], T.mm[:], ())
    dma("sn1a", "Y", T.snr[0:112, 1, :], T.sn[16:128, :], ())
    dma("sn1b", "S", T.snr[112:128, 1, :], T.sn[0:16, :], ())
    dma("h0", "S", T.hw0[:, 0:NV], T.h0[:], ())
    dma("pd", "Y", T.raw[:, 0, :, :], T.pd[:], ())
    dma("lb", "Y", T.raw[:, 1, :, :], T.lb[:], ())
    dma("ob", "Y", T.ob[:], T.obs[:], ())
    dma("th", "Y", T.tht[:, 0:1], T.th[:], ())
    dma("wv0", "Y", T.wav[:, 0:NA], T.wv[:], ())

    cf = T.cf
    gp("pi", lambda: g.iota(T.pi[:, 0:1], [[0, 1]], 0, 1), ())
    vm("zero", T.zero[:], 0.0)
    vm("tin0", T.tin[:], 0.0, ["tinA", "tinB", "tinAb", "tinBb"])
    gp("sh1", lambda: g.affine_select(T.sh1[:], T.zero[:], [[-1, 128]], ALU.not_equal, 1.0, -16, 1), ["zero"])
    gp("shb", lambda: g.affine_select(T.shb[:], T.sh1[:], [[-1, 128]], ALU.not_equal, 1.0, 112, 1), ["sh1"])
    gp("nat0", lambda: g.iota(T.nat0[:], [[1, 16], [512, 4]], 0, 0), ())
    gp("idb", lambda: g.affine_select(T.idb[:], T.zero[:], [[-1, 128]], ALU.not_equal, 1.0, 0, 1), ["zero"])
    gp("uu", lambda: g.iota(T.uu[:], [[1, 144]], 0, -1, allow_small_or_imprecise_dtypes=True), ())
    gp("kcol", lambda: g.iota(T.kc[:], [[1, 256]], 0, 0, allow_small_or_imprecise_dtypes=True), ())
    vs("ci0", T.ci[:, 0:1], T.pi[:, 0:1], 15, None, ALU.bitwise_and, None, ["pi"])
    vs("ci1", T.ci[:, 1:2], T.pi[:, 0:1], 4, 1, ALU.arith_shift_right, ALU.bitwise_and, ["pi"])
    vc("cf", cf[:, 0:2], T.ci[:, 0:2], ["ci0", "ci1"])
    vs("c32", cf[:, 2:3], cf[:, 0:1], 32.0, None, ALU.mult, None, ["cf"])
    vs("cpb", cf[:, 3:4], cf[:, 0:1], -16.0 * CUT, None, ALU.add, None, ["cf"])
    vs("c12", cf[:, 12:13], cf[:, 1:2], -1.0, 1.0, ALU.mult, ALU.add, ["cf"])
    vs("c6", cf[:, 6:7], cf[:, 0:1], -1.0, 15.0, ALU.mult, ALU.add, ["cf"])
    for j, wgt in enumerate((2.0 ** 22, 2.0 ** 30, 4.0, 1024.0)):
        vs("w%d" % j, cf[:, 7 + j:8 + j], cf[:, 0:1], float(j), wgt, ALU.is_equal, ALU.mult, ["cf"])
    vt("wm", cf[:, 13:14], cf[:, 7:8], cf[:, 8:9], ALU.add, ["w0", "w1"])
    vt("wp", cf[:, 14:15], cf[:, 9:10], cf[:, 10:11], ALU.add, ["w2", "w3"])
    copy("shf", T.shf[:], T.shb[:], ["shb"])
    copy("ident", T.ident[:], T.idb[:], ["idb"])
    act("id14", T.id14[:], T.idb[:], ACT.Identity, 0.0, 2.0 ** 14, ["idb"])
    vs("nat", T.nat[:], T.nat0[:], cf[:, 2:3], None, ALU.add, None, ["nat0", "c32"])

    peers = [T.cores[(rank + d) % NR] for d in range(1, NR)]

    def show_m(t, split):
        own = T.mwq if t == 0 else T["mw%d" % t]
        lst, base = (T.sn0, NV) if t == 0 else (T.snm, 2 * NV)
        for c0, c1, s, k in spans("tr", split):
            bs = slice(c0 // 4, c1 // 4)
            vc("tinA" + s, T.tin[:, bs, 0:4], T.dg[:, bs, :], k("dg0", "dg1", "dg2", "dg3"), k("tinA"))
            mm("sh" + s, [(T.hs2[:, c0:c1], T.shb[:], T.tin[:, bs, 0:4], True, True)], ["shb"] + k("tinA"), k("dsh"), ["hs2"])
            copy("tinB" + s, T.tin[:, bs, 16:20], T.hs2[:, c0:c1], k("dsh"), k("tinB"), ["hs2"])
            op("tr" + s, "V", lambda e, c0=c0, c1=c1, bs=bs: g.vector.transpose(own[:, 8 * c0:8 * c1], T.tin[:, bs, :]), k("tinA", "tinB"), k("tr%d" % t))
        r = ["tr%d" % t, "tr%db" % t, "sn0" if t == 0 else "snm"]
        for d in range(NR - 1):
            copy("ms%d" % d, T["msn%d" % t][:, 256 * d:256 * d + 256], own[:, 0:2048].indirect(lst[:, 16 * d:16 * d + 16]), r, ["msn%d_%d" % (t, d)])
        send("m", CALLS_M, T["msn%d" % t], T["mw%d" % t], base, t)
        if t == 0: copy("own", T.mw0[:, 0:NV], T.mwq[:].indirect(T.nat[:]), ["tr0", "nat"])

    def send(x, calls, src, dst, base, t):
        sem, n = "a%s%d" % (x, t), 0
        for c, ds in enumerate(calls):
            handed = [d for d in ds if x == "h" and d in HANDED]
            direct = [d for d in ds if d not in handed]
            def fn(e, handed=handed, direct=direct):
                trs, used = [], 0
                for d in direct + handed:
                    block = src[:, 256 * d:256 * d + 256]
                    if d in direct:
                        to, mine = peers[d], topo.engines(core, peers[d])[direct.index(d)::len(direct)]
                        land, arrive = dst[:, base + 256 * d:base + 256 * d + 256], sem
                    else:
                        to = helper(T, topo, rank, d)
                        mine, land, arrive = on_chip_engines(T, topo, rank, d)[handed.index(d)::len(handed)], block, "fw%d" % t
                    rid, pid, _ = topo.addr(to)
                    trs.append(RemoteDMATransfer(dst_ids=[DstId(rid=rid, pnc=pid)], dma_engine_mask=sum(1 << i for i in mine), remote_sem=T.sem[arrive],
                                                 src=block, dst=land))
                    used += len(mine)
                g.remote_dma_fused(trs, local_sem=T.sem.sent)
                return used
            s = op("send%s%d" % (x, c), "G", fn, ["%ssn%d_%d" % (x, t, d) for d in ds], kind="r")
            n += sum(len(topo.engines(T.cores[(rank - d - 1) % NR], core)) // len(direct) for d in direct)
            n += sum(len(topo.engines(helper(T, topo, (rank - d - 1) % NR, d), core)) for d in handed)
        op("got" + x, "", (sem, n), (), ["%sr%d" % (x, t)], kind="a", after=[s])

    def move(u, src, cols, name):
        if now[0] >= 0 and u in MOVE_BY_DMA:
            for x, (to, fro) in enumerate(((slice(0, 112), slice(16, 128)), (slice(112, 128), slice(0, 16)))):
                k = dma("hd%d%d" % (u, x), "Y", T.hmv[to, cols], src[fro, cols], [name], ["hm%d" % u + "x" * x])
                ops[k]["deps"].update(readers.get("snh", ()))
            return
        ps, hs = T.hs[:, u % 2, 0:cols.stop - cols.start], "hs%d" % (u % 2)
        mm("hs%d" % u, [(ps, T.shf[:], src[:, cols], True, True)], ["shf", name], [hs], [hs])
        k = copy("hc%d" % u, T.hmv[:, cols], ps, [hs], ["hm%d" % u], [hs])
        ops[k]["deps"].update(readers.get("snh", ()))

    def show_h(t, moved):
        for d in range(NR - 1):
            copy("hg%d" % d, T["hsn%d" % t][:, 256 * d:256 * d + 256], T.hmv[:].indirect(T.snh[:, 16 * d:16 * d + 16]), moved + ["snh"], ["hsn%d_%d" % (t, d)])
        send("h", CALLS_H, T["hsn%d" % t], T["hw%d" % t], NV, t)

    sr = ["sn1a", "sn1b"]
    vs("sq", T.snq[:, 0, :], T.snr[:, 1, :], 6, None, ALU.arith_shift_right, None, sr)
    vs("su", T.snf[:, 0, :], T.snq[:, 0, :], -2047.0 / 32, None, ALU.mult, None, ["sq"])
    vt("sv", T.snf[:, 1, :], T.snf[:, 0, :], T.snr[:, 1, :], ALU.add, ["su"] + sr)
    vs("sn0", T.sn0[:], T.snf[:, 1, :], 32.0, 16.0, ALU.mult, ALU.add, ["sv"])
    vs("dMl", T.dg[:, :, 0], T.mmi[:, 0, :], 255, None, ALU.bitwise_and, None, ["mt"], ["dg0"])
    vs("dMh", T.dg[:, :, 1], T.mmi[:, 0, :], 8, None, ALU.arith_shift_right, None, ["mt"], ["dg1"])
    vs("dml", T.dg[:, :, 2], T.mmi[:, 1, :], 255, None, ALU.bitwise_and, None, ["mm"], ["dg2"])
    vs("dmh", T.dg[:, :, 3], T.mmi[:, 1, :], 8, 3, ALU.arith_shift_right, ALU.bitwise_and, ["mm"], ["dg3"])
    show_m(0, ())
    vc("snh", T.snh[:], T.snr[:, 1, :], sr)
    for u in range(2): move(u, T.hw0, slice(512 * u, 512 * u + 512), "h0")
    show_h(0, ["hm0", "hm1"])

    for k in range(4):
        vc("prm%d" % k, T.prm[:, :, :, k], T.raw[:, :, k, :], ["pd", "lb"])
    pr = ["prm%d" % k for k in range(4)]
    vc("pdh", T.pdh[:], T.prm[:, 0, :, :], pr)
    vs("pct", T.pct[:], T.prm[:, 0, :, :], 1.0 / 2048, 0.5625, ALU.mult, ALU.add, pr)
    vt("pc", T.pc[:], T.pct[:], T.prm[:, 1, :, :], ALU.add, ["pct"] + pr)
    vs("pq0", T.pdq[:, 0, :, :], T.prm[:, 0, :, :], 2032, None, ALU.bitwise_and, None, pr)
    vs("pq1", T.pdq[:, 1, :, :], T.pdq[:, 0, :, :], 1024.0, None, ALU.min, None, ["pq0"])
    vt("pq2", T.pdq[:, 2, :, :], T.pdq[:, 1, :, :], T.prm[:, 0, :, :], ALU.add, ["pq1"] + pr)
    vc("pdm", T.pdm[:], T.pdq[:, 2, :, :], ["pq2"])
    vs("sm0", T.snq[:, 1, :], T.snr[:, 1, :], 2032, None, ALU.bitwise_and, None, sr)
    vt("sm1", T.snq[:, 2, :], T.snq[:, 1, :], T.snr[:, 1, :], ALU.add, ["sm0"] + sr)
    vs("snm", T.snm[:], T.snq[:, 2, :], 16.0, None, ALU.add, None, ["sm1"])
    vs("zp", T.zp[:], T.uu[:], cf[:, 6:7], cf[:, 14:15], ALU.is_equal, ALU.mult, ["uu", "c6", "wp"])
    vs("zm", T.zm[:], T.uu[:], cf[:, 6:7], cf[:, 13:14], ALU.is_equal, ALU.mult, ["uu", "c6", "wm"])
    vs("zc", T.zc[:], T.uu[:], cf[:, 6:7], 2.0 ** 22, ALU.is_equal, ALU.mult, ["uu", "c6"])
    vm("cen", T.cen[:], -64.0 * 256)
    vm("rst", T.rst[:], 0.0)
    vm("rs4", T.rst[:, 0::4], 1e20, ["rst"])
    act("ob8", T.ob8[:], T.ob[:], ACT.Identity, 0.0, 0.125, ["ob"])
    act("nth", T.tht[:, 1:2], T.tht[:, 0:1], ACT.Identity, 0.0, -1.0, ["th"])

    def extract(z, src, out, q, stop):
        c0, c1 = chunks[q]
        return [(out, z[:, 15 - i:143 - i], src[:, 16 * c0 + i:16 * c1:16], False, stop and i == 15) for i in range(16)]

    def keycols(c0, c1):
        return (T.key[:, c0:c1], "key") if c0 < CUT else (T.pay[:, 3, 256 + c0 - CUT:256 + c1 - CUT], "pay3")

    def start_key(c0, c1, s, t):
        key, bank = keycols(c0, c1)
        mm("kc" + s, [(key, T.id14[:], T.kc[:, c0:c1], True, False)] + ([(key, T.id14[:], T.cen[:, c0:c1], False, False)] if t == 0 else []),
           ["id14", "kcol", "cen"], within("key", c0, c1), [bank])

    for t in range(NT):
        now[0] = t
        hw, mw = T["hw%d" % t], T["mw%d" % t]
        last = t == NT - 1
        start_key(0, CUT, "", t)
        for q, (c0, c1) in enumerate(chunks):
            k, bank, cs, js = str(q), "pay%d" % (c0 // 64), slice(c0, c1), slice(16 * c0, 16 * c1)
            pay = T.pay[:, c0 // 64, c0 % 64:c0 % 64 + c1 - c0]
            if t == 0: copy("dig" + k, T.g2[:, js], mw[:, 0:1792].indirect(T.pdh[:, cs]), ["own", "mr0", "pdh"])
            else: copy("dig" + k, T.g2[:, js], mw[:].indirect(T.pdm[:, cs]), ["tr%d" % t, "tr%db" % t, "mr%d" % t, "pdm"])
            mm("pc" + k, [(pay, T.ident[:], T.pc[:, cs], True, False)], ["ident", "pc"], ["pay" + k, "grp" + bank], [bank])
            mm("xa" + k, extract(T.zp, T.g2, pay, q, True), ["zp", "dig" + k], ["pay" + k, "grp" + bank], [bank])
            if t == 0:
                vs("ai" + k, T.ai[:, 0, cs], pay, MAGIC, MAGIC + 1, ALU.add, ALU.subtract, ["pay" + k], None, [bank])
                vs("am" + k, T.ai[:, 1, cs], T.ai[:, 0, cs], NA - 1, None, ALU.bitwise_and, None, ["ai" + k])
                vc("al" + k, T.al[:, cs], T.ai[:, 1, cs], ["am" + k])
            else:
                vs("al" + k, T.al[:, cs], pay, MAGIC, MAGIC + 1, ALU.add, ALU.subtract, ["pay" + k], None, [bank])
            win = T.wav[:, 0:NA] if t == 0 else T.wav[:]
            copy("wg" + k, T.wb[:, js], win.indirect(T.al[:, cs]), ["wv0", "al" + k] + ([] if t == 0 else ["wv1"]))
        start_key(CUT, 256, "b", t)
        for q, (c0, c1) in enumerate(chunks):
            mm("xm%d" % q, extract(T.zm, T.g2, keycols(c0, c1)[0], q, False), ["zm", "dig%d" % q], ["key%d" % q], [keycols(c0, c1)[1]])
        if t == 0:
            dma("wv1", "Y", T.wav[:, NA:2 * NA], T.wv[:], ["hr0"])
        for q, (c0, c1) in enumerate(chunks):
            k, js = str(q), slice(16 * c0, 16 * c1)
            if q in H_ON_SCALAR:
                n = 16 * (c1 - c0)
                copy("hq" + k, T.hq[:, 0:n], hw[:].indirect(T.pdh[:, c0:c1]), hk(t) + ["hr%d" % t, "pdh"], ["hq"])
                mm("wq" + k, [(T.hs[:, b, :], T.idb[:], T.wb[:, 16 * c0 + 512 * b:16 * c0 + 512 * b + 512], True, True) for b in range(n // 512)],
                   ["idb", "wg" + k], ["hs0", "hs1"], ["hs0", "hs1"])
                vt("pr" + k, T.prod[:, js], T.hs[:, 0:n // 512, :], T.hq[:, 0:n], ALU.mult, ["hq", "hs0", "hs1"], None, ["hs0", "hs1"])
            else:
                vt("pr" + k, T.prod[:, js], hw[:].indirect(T.pdh[:, c0:c1]), T.wb[:, js], ALU.mult, hk(t) + ["hr%d" % t, "pdh", "wg" + k])
            act("ab" + k, T.ab[:, js], T.prod[:, js], ACT.Abs, T.ob[:, t:t + 1], -1.0, ["pr" + k, "ob"])
            if q in ON_SCALAR[last]:
                act("sg" + k, T.sg[:, js], T.ab[:, js], ACT.Sign, T.tht[:, 1:2], 1.0, ["ab" + k, "nth"])
                act("cm" + k, T.cmp[:, js], T.sg[:, js], ACT.Relu, 0.0, 1.0, ["sg" + k])
            else:
                vs("cm" + k, T.cmp[:, js], T.ab[:, js], T.tht[:, 0:1], None, ALU.is_gt, None, ["ab" + k, "th"])
            (key, bank), end = keycols(c0, c1), k == CLOSE or c1 == 256
            mm("xc" + k, extract(T.zc, T.cmp, key, q, end), ["zc", "cm" + k], ["key" + k], [bank])
        for a, b in ((0, CUT), (CUT, 256)):
            group = [j for j, o in enumerate(ops) if o["name"] in [(t, nm) for nm in within("xc", a, b) + within("xm", a, b)]]
            close = [j for j in group if ops[j]["name"][1] == ("xc" + CLOSE if a == 0 else within("xc", a, b)[-1])][0]
            ops[close]["deps"].update(j for j in group if j != close)
            for nm in within("key", a, b): lastw[nm] = close
        split = SPLIT_LAST if last else SPLIT
        def scan(name, out, d0, d1, o0, o1, r, w, banks):
            op(name, "V", lambda e: g.vector.tensor_tensor_scan(out, d0, d1, 0.0, o0, o1), r, w, banks)
        for c0, c1, s, k in spans("rr", split):
            key, bank = keycols(c0, c1)
            scan("rr" + s, T.rr[:, c0:c1], T.rst[:, c0:c1], key, ALU.add, ALU.min, within("key", c0, c1) + ["rst"], k("rr"), [bank])
            vt("dd" + s, T.dd[:, c0:c1], key, T.rr[:, c0:c1], ALU.subtract, within("key", c0, c1) + k("rr"), k("dd"), [bank])
        for c0, c1, s, k in spans("d1", split):
            vt("d1" + s, T.d1[:, c0:c1], T.pay[:, c0 // 64:c1 // 64, 0:64], T.dd[:, c0:c1], ALU.subtract, within("pay", c0, c1) + k("dd"), k("d1"),
               ["pay%d" % b for b in range(c0 // 64, c1 // 64)])
            scan("ss" + s, T.ss[:, c0:c1], T.dd[:, c0:c1], T.d1[:, c0:c1], ALU.min, ALU.max, k("dd", "d1"), k("ss"), ())
        for c0, c1, s, k in spans("pk", split):
            bs = slice(c0 // 4, c1 // 4)
            vs("x0" + s, T.xx[:, bs, 0], T.rr[:, c0 + 3:c1:4], 2.0 ** -11, None, ALU.mult, None, k("rr"), k("x0"))
            vs("pk1" + s, T.lq[:, 0, bs], T.xx[:, bs, 0], 2040, None, ALU.bitwise_and, None, k("x0"), k("pk1"))
            vs("pk" + s, T.lu[:, bs], T.lq[:, 0, bs], 2.0, cf[:, 3:4] if c0 else cf[:, 0:1], ALU.mult, ALU.add, k("pk1") + ["cf", "cpb"], k("pk"))
        for c0, c1, s, k in spans("pd", split):
            bs = slice(c0 // 4, c1 // 4)
            vs("x1" + s, T.xx[:, bs, 1], T.ss[:, c0 + 3:c1:4], 2048.0, -1152.0, ALU.mult, ALU.add, k("ss"), k("x1"))
            vs("pd1" + s, T.lq[:, 1, bs], T.xx[:, bs, 1], 2047, None, ALU.bitwise_and, None, k("x1"), k("pd1"))
            vc("pdl" + s, T.lu[:, 64 + c0 // 4:64 + c1 // 4], T.lq[:, 1, bs], k("pd1"), k("pdl"))
        if not last:
            for c0, c1, s, k in spans("dg", split):
                bs = slice(c0 // 4, c1 // 4)
                vs("dlo" + s, T.dg[:, bs, 0::2], T.xx[:, bs, :], 11, 255, ALU.arith_shift_right, ALU.bitwise_and, k("x0", "x1"), k("dg0", "dg2"))
                vs("dMh" + s, T.dg[:, bs, 1], T.xx[:, bs, 0], 19, None, ALU.arith_shift_right, None, k("x0"), k("dg1"))
                vs("dmh" + s, T.dg[:, bs, 3], T.xx[:, bs, 1], 19, 3, ALU.arith_shift_right, ALU.bitwise_and, k("x1"), k("dg3"))
            show_m(t + 1, split)
        for u, (u0, u1) in enumerate(cuts(LAST_PIECES if last else PIECES)):
            c0, c1, s, k = [x for x in spans("pk", split) if x[0] <= 4 * u0 < x[1]][0]
            kd = [x for x in spans("pd", split) if x[0] <= 4 * u0 < x[1]][0][3]
            pick, pds = T.lu[:, u0:u1], T.lu[:, 64 + u0:64 + u1]
            vsl, ws, su = slice(16 * u0, 16 * u1), slice(16 * c0, 16 * c1), str(u)
            free = hk(t)
            act("ep" + su, T.ep[:, vsl], T.prod[:, ws].indirect(pick), ACT.Identity, T.ob8[:, t:t + 1], -0.125, within("pr", c0, c1) + k("pk") + ["ob8"] + free)
            dst = T.hout if last else T["hw%d" % (t + 1)]
            new, mode = "h%d_%d" % (t + 1, u), VIA_PSUM[last][u]
            ps, bank = T.pay[:, u, 0:16 * (u1 - u0)], ["pay" + su]
            if mode == 0:
                vt("tb" + su, T.tb[:, vsl], T.wb[:, ws].indirect(pick), T.ep[:, vsl], ALU.mult, within("wg", c0, c1) + k("pk") + ["ep" + su] + free)
            else:
                copy("ws" + su, T.wsl[:, vsl], T.wb[:, ws].indirect(pick), within("wg", c0, c1) + k("pk") + free)
                mm("wp" + su, [(ps, T.idb[:], T.wsl[:, vsl], True, True)], ["idb", "ws" + su], ["pay" + su], bank)
                vt("tb" + su, ps if mode == 2 else T.tb[:, vsl], ps, T.ep[:, vsl], ALU.mult, ["pay" + su, "ep" + su] + free,
                   ["tb" + su, "pay" + su] if mode == 2 else None, bank)
            if mode < 2:
                vt("hn" + su, dst[:, vsl], hw[:].indirect(pds), T.tb[:, vsl], ALU.add, hk(t) + ["hr%d" % t, "tb" + su] + kd("pdl"), [new])
            else:
                copy("hp" + su, T.tb[:, vsl], hw[:].indirect(pds), hk(t) + ["hr%d" % t] + kd("pdl") + free)
                vt("hn" + su, dst[:, vsl], ps, T.tb[:, vsl], ALU.add, ["hp" + su, "tb" + su, "pay" + su], [new], bank)
            if last:
                dma("yh" + su, "Y", T.yh[:, vsl], T.hout[:, vsl], [new])
            else:
                move(u, dst, vsl, new)
        if not last:
            show_h(t + 1, ["hm%d" % u + x for u in range(len(PIECES)) for x in ("", "x")])

    vs("xM", T.xp[:, 0, :], T.xx[:, :, 0], 11, None, ALU.arith_shift_right, None, ["x0", "x0b"])
    vs("xm", T.xp[:, 1, :], T.xx[:, :, 1], 11, NA - 1, ALU.arith_shift_right, ALU.bitwise_and, ["x1", "x1b"])
    vs("fM", T.ff[:, 0, :], T.xp[:, 0, :], 64.0, None, ALU.add, None, ["xM"])
    vc("fm", T.ff[:, 1, :], T.xp[:, 1, :], ["xm"])
    for b in range(4):
        for x, col in enumerate((cf[:, 12:13], cf[:, 1:2])):
            def fn(e, b=b, x=x, col=col):
                if e == "V": return g.vector.tensor_scalar(T.t2i[:, b::4, x, :], T.ff[:, :, b::4], col, None, ALU.mult)
                return g.scalar.activation(T.t2i[:, b::4, x, :], T.ff[:, :, b::4], ACT.Identity, scale=col)
            op("tj%d" % (2 * b + x), "VS", fn, ["fM", "fm", "c12", "cf"], ["tj%d" % (2 * b + x)])
    op("t2", "V", lambda e: g.vector.transpose(T.t2o[:], T.t2i[:]), ["tj%d" % j for j in range(8)], ["t2"])
    vt("no", T.no[:], T.t2o[:, :, 0, :], T.t2o[:, :, 1, :], ALU.add, ["t2"])
    dma("ymt", "Y", T.ymt[:], T.no[:, 0:4, :], ["no"])
    dma("ymm", "S", T.ymm[:], T.no[:, 4:8, :], ["no"])
    return ops


def queues(ops, order):
    at = {o["name"]: k for k, o in enumerate(ops)}
    qs = {e: [] for e in "VSPGY"}
    for k, o in enumerate(ops):
        if o["kind"] == "d" and o["engs"] == "S" and o["name"][0] < 0: qs["S"].append(k)
        if o["engs"] in ("G", "Y"): qs[o["engs"]].append(k)
    for e, (start, step, last) in order.items():
        for t in range(-1, NT):
            for nm in (start if t < 0 else step if t < NT - 1 else last).split():
                k = at.get((t - nm.endswith("-"), nm.rstrip("-")))
                if k is not None and not (t == 0 and nm.endswith("-")): qs[e].append(k)
    qs["S"].append(at[(NT - 1, "ymm")])
    return qs


def emit(g, T, ops, qs):
    queue = {"V": g.vector, "S": g.scalar, "P": g.tensor, "G": g, "Y": g.sync}
    qsem = {"V": "qv", "S": "qs", "P": "qp", "G": "qg"}
    seq, done, head = [], set(), {e: 0 for e in qs}
    arrivals = [k for k, o in enumerate(ops) if o["kind"] == "a"]
    while len(seq) < len(ops):
        ready = [(k, "") for k in arrivals if k not in done] + [(qs[e][head[e]], e) for e in qs if head[e] < len(qs[e])]
        k, e = [(k, e) for k, e in ready if ops[k]["deps"] <= done][0]
        seq.append(k); done.add(k); ops[k]["eng"] = e
        if e: head[e] += 1
    place = {k: i for i, k in enumerate(seq)}
    pos, cnt, ndma = {}, {e: 0 for e in queue}, 0
    known = {e: {} for e in queue}
    snap, waits, need = {}, {}, set()
    for k in seq:
        o = ops[k]
        if o["kind"] == "a":
            pos[k] = (o["fn"][0], 1); snap[k] = {o["fn"][0]: 1}; continue
        e = o["eng"]; kn = known[e]; w = []
        for d in sorted(o["deps"], key=lambda d: -place[d]):
            od = ops[d]
            if od["kind"] == "r" or (e == "P" and od["eng"] == "P"): continue
            s, v = pos[d]
            if kn.get(s, 0) >= v: continue
            w.append(d); need.add(d)
            for s2, v2 in snap[d].items():
                if kn.get(s2, 0) < v2: kn[s2] = v2
        waits[k] = w
        if o["kind"] == "d":
            pos[k] = ("dm%d" % ndma, 1); ndma += 1
        elif o["kind"] == "c":
            cnt[e] += 1; pos[k] = (qsem[e], cnt[e])
        if o["kind"] != "r":
            snap[k] = dict(kn); snap[k][pos[k][0]] = pos[k][1]
    val, tot, waited = {}, {}, {}
    for k in seq:
        o = ops[k]
        if o["kind"] == "a":
            val[k] = o["fn"]; tot[o["fn"][0]] = o["fn"][1]; continue
        e = o["eng"]
        for d in waits[k]:
            s, v = val[d]
            queue[e].wait_ge(T.sem[s], v); waited[s] = max(waited.get(s, 0), v)
        ins = o["fn"](e)
        if o["kind"] == "r":
            tot["sent"] = tot.get("sent", 0) + ins
        elif o["kind"] == "d":
            s = pos[k][0]; ins.then_inc(T.sem[s], 16); val[k] = (s, 16); tot[s] = 16
        elif k in need:
            s = qsem[e]; tot[s] = tot.get(s, 0) + 1; ins.then_inc(T.sem[s], 1); val[k] = (s, tot[s])
    for s, v in tot.items():
        if waited.get(s, 0) < v: g.wait_ge(T.sem[s], v)


def rank_program(g, core, T, topo):
    if T.rank_of(core) is None:
        for rank in range(NR):
            for d in HANDED:
                if helper(T, topo, rank, d) == core: hand_on(g, core, T, topo, rank, d)
        return
    ops = plan(g, core, T, topo)
    emit(g, T, ops, queues(ops, ORDER))
